import numpy as np, ml_dtypes
CORES = [48,51,52,55]
N = 4
BF = ml_dtypes.bfloat16
def gentries(a):
    return np.ascontiguousarray(a.reshape(8, 16, -1).transpose(0, 2, 1)).reshape(8, -1)
def gtable(e):
    e = np.asarray(e); return np.ascontiguousarray(e.reshape(8, -1, 16).transpose(0, 2, 1)).reshape(128, -1).astype(np.int32)
V, D, L, CAP, RO = 4096, 4, 4, 256, 2
K = V // 256
def pack(w, z, cd):
    return {"wish": np.ascontiguousarray(w.reshape(N, 128, V)).astype(np.float32).astype(BF), "goods": np.ascontiguousarray(z.reshape(N, 128, V)).astype(np.float32).astype(BF),
            "cand": np.stack([gtable(a.reshape(8, -1)) for a in cd])}
def ring(o, m):
    a = o[:len(o) // m * m].reshape(-1, m)
    return a, np.roll(a, -1, axis=1)
def lead(rng, w, z, cd, q, g, a, b):
    w[q, g][:, a] = z[q, g][:, b]; cd[q, g][rng.integers(0, D, a.shape), a] = b
def coded(rng):
    h = rng.integers(0, 256, (N, 8, 8, V)); n = np.argsort(rng.random((N, 8, V)), axis=-1)
    h[:, :, 0] = n & 255; h[:, :, 1] = n >> 8
    return np.concatenate([h, 255 - h], axis=2)
def part(rng, z):
    return (z * rng.random(z.shape)).astype(np.int64)
def twice(rng, w, z, cd, q, g, o):
    a, b = ring(o, L); n = len(a); x = np.arange(n)[:, None]; j = np.arange(L)[None, :]
    c = np.argsort(rng.random((n, 16)), axis=1)[:, :L]
    lo = rng.integers(0, 2, (n, L)); st = np.where(rng.random((n, 1, 1)) < 0.5, 1, rng.integers(1, 127, (n, L, 2)))
    zz = rng.integers(0, 4, (n, 1, 16)) + np.zeros((n, L, 16), np.int64); ww = np.full((n, L, 16), 255)
    for k in range(L):
        zz[x, (j + k) % L, c] = (lo, lo + st[:, :, 0], lo + st[:, :, 0] + st[:, :, 1])[k] if k < 3 else lo
        if k: ww[x, (j + k) % L, c] = 0
    z[q, g][:, a] = zz.transpose(2, 0, 1); w[q, g][:, a] = ww.transpose(2, 0, 1)
    cd[q, g][:, a] = np.where(rng.random((D,) + a.shape) < 0.5, a, b); cd[q, g][rng.integers(0, D, a.shape), a] = b
def calm(rng, w, z, cd, g):
    sets = []
    for q in range(N):
        o = rng.permutation(V); n = int(rng.integers(2, CAP + 1))
        sets.append((n, np.concatenate([np.sort(o[:n]), np.sort(o[n:])])))
    for q in range(N):
        n, s = sets[q]; k = s[:CAP]; come = z[q - 1, g][:, sets[q - 1][1][:CAP]]
        w[q, g][:, k] = part(rng, np.minimum(z[q, g][:, k], come)); w[q, g][:, s[:n]] = come[:, :n]
        v = rng.permutation(s[CAP:])[:n]
        z[q, g][:, v] = come[:, :n]; w[q, g][:, v] = part(rng, come[:, :n])
        cd[q, g][rng.integers(0, D, n), s[:n]] = v
def plant(rng, w, z, cd):
    for q in range(N):
        share = rng.permutation(np.array([0.01, 0.05, 0.3, 0.9, 0.01, 0.1, 0.5, 0.9]))
        for g in range(8):
            o = rng.permutation(V); i = 0
            for m in range(2, L + 2):
                a, b = ring(o[i:i + m * K], m); i += m * K
                lead(rng, w, z, cd, q, g, a, b)
                w[q, g][:, a] = np.clip(w[q, g][:, a] + rng.integers(-3, 2, (16,) + a.shape), 0, 255)
            p = o[i:i + RO * K].reshape(RO, K); i += RO * K
            u = o[i:i + RO * K].reshape(RO, K); i += RO * K
            for j in range(RO):
                s = rng.permutation(D); v = u[max(j - 1, 0)]
                if j: z[q, g][:, u[j]] = np.maximum(z[q, g][:, v] - rng.integers(0, 4, (16, K)), 0)
                w[q, g][:, p[j]] = z[q, g][:, v]; w[q, g][:, u[j]] = z[q, g][:, p[j]]
                cd[q, g][s[0], p[j]] = v; cd[q, g][s[1], p[j]] = u[j]; cd[q, g][s[2], u[j]] = p[j]
            r = o[i:]; r = r[rng.random(len(r)) >= share[g]]
            w[q, g][:, r] = part(rng, z[q, g][:, r])
    return pack(w, z, cd)
def setup_inputs(rng):
    z = rng.integers(0, 256, (N, 8, 16, V)); w = rng.integers(0, 256, (N, 8, 16, V)); cd = rng.integers(0, V, (N, 8, D, V))
    return plant(rng, w, z, cd)
def setup_inputs_room(rng):
    z = coded(rng); w = part(rng, z); cd = rng.integers(0, V, (N, 8, D, V))
    for q in range(N):
        for g in range(8):
            n = int(rng.choice(np.array([0, 1, CAP - 1, CAP, CAP + 1, V // 2])))
            if q < 2: n = (CAP, CAP + 1, CAP - 1, 1, 0, V // 2, CAP, CAP + 1)[(g + q) % 8]
            o = rng.permutation(V); i = n
            if q < 2 and n:
                j = int(np.flatnonzero(o == V - 1)[0]); o[j] = o[0]; o[0] = V - 1
            lead(rng, w, z, cd, q, g, o[:n], rng.choice(o[n:], n))
            for m in range(2, L + 1):
                a, b = ring(o[i:i + m * K], m); i += m * K
                lead(rng, w, z, cd, q, g, a, b)
    return pack(w, z, cd)
def setup_inputs_rings(rng):
    z = coded(rng); w = part(rng, z); cd = rng.integers(0, V, (N, 8, D, V)); far = int(np.lcm.reduce(np.arange(1, L + 1)))
    calm(rng, w, z, cd, 5)
    for q in range(N):
        for g in range(8):
            if g == 5: continue
            if g == 4:
                w[q, g][:, :CAP] = 0
                twice(rng, w, z, cd, q, g, CAP + rng.permutation(V - CAP)); continue
            ms = [[L + 1], [2], [3], [L]][g] if g < 4 else [int(m) for m in rng.permutation(np.array(list(range(1, L + 3)) + [2 * L, 3 * L, far]))]
            o = rng.permutation(V); n = V // sum(ms); i = 0
            for m in ms:
                a, b = ring(o[i:i + n * m], m); i += n * m
                lead(rng, w, z, cd, q, g, a, b)
            if i < V:
                a, b = ring(o[i:], V - i); lead(rng, w, z, cd, q, g, a, b)
    return pack(w, z, cd)
def setup_inputs_ties(rng):
    z = np.zeros((N, 8, 16, V), np.int64); w = np.zeros((N, 8, 16, V), np.int64); cd = np.zeros((N, 8, D, V), np.int64); h = V // 2; t = V // 4
    for q in range(N):
        for g in range(8):
            o = rng.permutation(V); lo, hi = o[:h], o[h:]
            bl = np.concatenate([rng.integers(0, 61, 12), np.full(4, 255)]); bh = rng.integers(150, 255, 16)
            tl = np.stack([rng.permutation(bl) for _ in range(5)], axis=1); th = np.stack([rng.permutation(bh) for _ in range(5)], axis=1)
            zz, ww, cc = z[q, g], w[q, g], cd[q, g]
            zz[:, lo] = tl[:, rng.integers(0, 5, h)]; zz[:, hi] = th[:, rng.integers(0, 5, h)]
            cc[:, :] = rng.choice(lo, (D, V))
            a, b = lo[:t], hi[:t]; three = rng.random(t) < 0.5
            ww[:, a] = 255; ww[:, b] = zz[:, a]; cc[0, b] = a
            cc[D - 1, a] = np.where(rng.random(t) < 0.5, a, cc[D - 1, a])
            p = np.argsort(rng.random((t, D)), axis=1); x = np.sort(p[:, :3], axis=1); x2 = np.sort(p[:, :2], axis=1)
            x[~three] = x2[~three][:, [0, 1, 1]]
            which = np.where(three, rng.integers(0, 3, t), rng.integers(0, 2, t))
            v = np.where(np.arange(3)[:, None] == which[None, :], b[None, :], rng.choice(hi, (3, t))); v[2] = np.where(three, v[2], v[1])
            for i in range(3): cc[x[:, i], a] = v[i]
            e = hi[t:]; ww[:, e] = 255; cc[:, e] = np.roll(e.reshape(-1, 2), 1, axis=1).reshape(-1)[None, :]
            c = lo[t:]; ww[:, c] = np.concatenate([tl, th], axis=1)[:, rng.integers(0, 10, len(c))]
            cc[:, c] = rng.integers(0, V, (D, len(c))); cc[0, c] = np.where(rng.random(len(c)) < 0.3, c, cc[0, c]); cc[2, c] = np.where(rng.random(len(c)) < 0.5, cc[0, c], cc[2, c])
    return pack(w, z, cd)
def setup_inputs_ends(rng):
    z = rng.integers(0, 256, (N, 8, 16, V)); w = rng.integers(0, 256, (N, 8, 16, V)); cd = rng.integers(0, V, (N, 8, D, V))
    cd[:, ::2] = rng.choice(np.array([0, V - 1, V // 2, 3]), (N, 4, D, V))
    m = np.arange(V) ^ 1; m = np.where(rng.random(V) < 0.5, m, m[::-1])
    cd[:, 1::2, D - 1] = m; w[:, 1::2] = z[:, 1::2][:, :, :, m]
    w[:, 3::4] = part(rng, z[:, 3::4])
    w[:, 3::4, :, V - 1 - CAP // 2:V - 1] = z[:, 3::4, :, V // 2:V // 2 + 1]; cd[:, 3::4, 1, V - 1 - CAP // 2:V - 1] = V // 2
    w[..., 0] = z[..., V - 1]; w[..., V - 1] = z[..., 0]; cd[:, :, 0, 0] = V - 1; cd[:, :, 0, V - 1] = 0
    return pack(w, z, cd)
def setup_inputs_spread(rng):
    z = np.minimum((np.exp2(8 * rng.random((N, 8, 1, V))) * rng.random((N, 8, 16, V))).astype(np.int64), 255)
    w = np.minimum((np.exp2(8 * rng.random((N, 8, 1, V))) * rng.random((N, 8, 16, V))).astype(np.int64), 255)
    return plant(rng, w, z, rng.integers(0, V, (N, 8, D, V)))
def check_inputs(d):
    bad = []
    for k in ("wish", "goods"):
        v = d[k].astype(np.float32)
        if not np.all((v >= 0) & (v <= 255) & (v == np.floor(v))): bad.append("values of " + k)
    if np.min(d["cand"]) < 0 or np.max(d["cand"]) > V - 1: bad.append("range of cand")
    return bad
def reference(wish, goods, cand):
    w = wish.astype(np.float32).astype(np.int32).reshape(N, 8, 16, V); z = goods.astype(np.float32).astype(np.int32).reshape(N, 8, 16, V)
    cd = np.stack([gentries(a) for a in cand]).astype(np.int64).reshape(N, 8, D, V)
    own = np.zeros((N, 8, V), np.int64) + np.arange(V)
    for t in range(RO):
        best = np.add.reduce(np.maximum(w - z, 0), axis=2); f = own
        for d in range(D):
            c = cd[:, :, d]; s = np.add.reduce(np.maximum(w - np.take_along_axis(z, c[:, :, None, :], 3), 0), axis=2)
            f = np.where(s < best, c, f); best = np.minimum(s, best)
        h = f; back = np.zeros((N, 8, V), bool)
        for i in range(2, L + 1):
            h = np.take_along_axis(f, h, 2); back = back | (h == own)
        trade = (f != own) & back; unmet = (f != own) & ~back
        z = np.take_along_axis(z, np.where(trade, f, own)[:, :, None, :], 3)
        order = np.argsort(~unmet, axis=2, kind="stable")[:, :, None, :CAP]
        away = np.take_along_axis(z, order, 3)
        np.put_along_axis(z, np.broadcast_to(order, (N, 8, 16, CAP)), np.roll(away, 1 + t, axis=0), 3)
    return {"y": z.reshape(N, 128, V).astype(np.float32).astype(BF)}

@@ -1,0 +1,541 @@
+from concourse.bass import DstId, RemoteDMATransfer
+from concourse.mybir import AluOpType as A, ActivationFunctionType as AF
+
+V = 4096
+FOLDS = (("o2", "o3", "o0", "o1"), ("o2", "o3", "o0", "o1"))
+PRE = 0
+WB = (0, 512, 1024, 2048, 3072, V)
+CUTS = (1280, 1792)
+G2 = (512, 512, 448, 320)
+ZS = 2944
+
+BF, F32, I32, U16 = "bfloat16", "float32", "int32", "uint16"
+SCRATCH = {"ps": ("psum", [128, 4096], F32)}
+for _dt, _names in (
+        (BF, "z0:4352 z1:4352 z2:4096 w:4096 chi:1024 clo:1024 x0:4096 x1:4096 x3:4096 x20:4096 x21:4096 xo0:4096 xo1:4096 "
+             "zg2:4096 zg3:4096 t2:4096 t3:4096 whi:256 wlo:256 hl:512 fh:256 fl:256 fi:512 nn:512 ft:256 eb:288 pin:272 "
+             "c256:272 tb:16 m1:256 s1:256 m2:256 m3:256 away0:256 away1:256 land0:256 land1:256 ahi:256 alo:256 k1:256 "
+             "k1a:256 kp:256 kpa:256 xg:128 con:128 coo:128 one:128 e1:128 en1:256 e16:128 en16:256 e256:128 e17:128 "
+             "e272:128 bd:128 nbd:128 ge:128 tri:128 ntri:128 gp:8 gn:8 sxy:16 s1w:144 s3w:144 s4w:144"),
+        (F32, "b0:256 di:512 pp:512 col:16"),
+        (I32, "ci:1024 bi:256 bj:256 hli:512 oi:16 oj:16 pi:2"),
+        (U16, "cu:1024 lf:256 lg:256 lp:256 l1:16 l2:16 l3:16 lv:16 lo:16")):
+    for _x in _names.split():
+        SCRATCH[_x.split(":")[0]] = ("sbuf", [128, int(_x.split(":")[1])], _dt)
+SEMAPHORES = (["pe", "dve", "act", "pool", "arr0", "arr1", "sent", "dc", "dz", "da0", "db0", "da1", "db1",
+               "dh0", "dl0", "dh1", "dl1", "dy0", "dy1"] + ["dw%d" % q for q in range(len(WB) - 1)]
+              + [p + f + str(t) for p in ("out", "back") for t in range(2) for f in FOLDS[t]])
+
+CY, GA, SC, PC, WAKE, DLAT, DRATE = 0.00095, 1.55, 3.5, 0.00048, 0.12, 2.0, 200e3
+
+
+def helpers(T, topo):
+    out, used = {}, set(T.cores)
+    for c in T.cores:
+        h = [x for x in topo.cores_of(c) if x not in used and topo.die(x) == topo.die(c)][0]
+        used.add(h)
+        out[c] = h
+    return out
+
+
+def folded(f, t):
+    return ("xo%d" if f[0] == "o" else "x2%d") % t, int(f[1]) * 1024, int(f[1]) * 1024 + 1024
+
+
+def plan(T, topo, core):
+    ops = []
+    rank = T.rank_of(core)
+    n_ranks = len(T.cores)
+    ps = T.ps
+
+    def add(q, fn, rd, wr, cost, sem=None, lat=0.0, inc=16, prio=1):
+        ops.append({"q": q, "fn": fn, "rd": rd, "wr": wr, "cost": cost, "sem": sem, "lat": lat, "inc": inc, "prio": prio})
+
+    def R(name, a=0, b=1 << 20):
+        return (name, a, b)
+
+    def P(a, n):
+        return ("ps", a, a + n)
+
+    def S(name, a=None, b=None, s=None):
+        return T[name][:, a:b:s]
+
+    def dve(fn, rd, wr, cyc):
+        add("dve", fn, rd, wr, 0.06 + max(cyc, 64) * CY)
+
+    def pe(mms, rd, wr, prio=1):
+        def fn(g):
+            last = None
+            for m in mms:
+                last = g.tensor.matmul(m[0], m[1], m[2], m[3], m[4])
+            return last
+        add("pe", fn, rd, wr, 0.03 + sum(max(64, m[5]) for m in mms) * PC, prio=prio)
+
+    def dma(q, sem, out, in_, rd, wr, nbytes):
+        add(q, lambda g: (g.sync if q == "sp" else g.scalar).dma_start(out, in_), rd, wr, 0.05, sem=sem, lat=nbytes / DRATE)
+
+    def ts(out, in0, s1, s2, op0, op1, rd, wr, cyc):
+        if op1 is None:
+            dve(lambda g: g.vector.tensor_scalar(out, in0, s1, None, op0), rd, wr, cyc)
+        else:
+            dve(lambda g: g.vector.tensor_scalar(out, in0, s1, s2, op0, op1), rd, wr, cyc)
+
+    def tt(out, in0, in1, op, rd, wr, cyc):
+        dve(lambda g: g.vector.tensor_tensor(out, in0, in1, op), rd, wr, cyc)
+
+    def cp(out, in_, rd, wr, cyc):
+        dve(lambda g: g.vector.tensor_copy(out, in_), rd, wr, cyc)
+
+    def scan(out, d0, d1, op0, op1, rd, wr, cyc):
+        dve(lambda g: g.vector.tensor_tensor_scan(out, d0, d1, 0.0, op0, op1), rd, wr, cyc)
+
+    def fill(name, val, a=None, b=None, cyc=64):
+        dve(lambda g: g.vector.memset(S(name, a, b), val), [], [R(name, a or 0, b or 1 << 20)], cyc)
+
+    def ac(out, in_, func, rd, wr, cyc, scale=1.0):
+        add("act", lambda g: g.scalar.activation(out, in_, func, scale=scale), rd, wr, 0.07 + max(cyc, 64) * CY)
+
+    def iota(out, pat, base, cm, wr, n, small=True):
+        if small:
+            add("pool", lambda g: g.iota(out, pat, base, cm, allow_small_or_imprecise_dtypes=True), [], wr, 0.13 + 2 * n * CY)
+        else:
+            add("pool", lambda g: g.iota(out, pat, base, cm), [], wr, 0.13 + 2 * n * CY)
+
+    def ind(win, n, lst, a, b):
+        return T[win][:, 0:n].indirect(T[lst][:, a // 16:b // 16])
+
+    def blocks(a, b, n=1024):
+        return [(o, min(o + n, b)) for o in range(a, b, n)]
+
+    wb = list(zip(WB[:-1], WB[1:]))
+    dma("sp", "dc", S("ci"), T.cand[:], [], [R("ci")], 512e3)
+    for q, (a, b) in enumerate(wb):
+        dma("sp", "dw%d" % q, S("w", a, b), T.wish[:, a:b], [], [R("w", a, b)], 256.0 * (b - a))
+        if q == 0:
+            dma("sp", "dz", S("z0", 0, V), T.goods[:], [], [R("z0", 0, V)], 1024e3)
+
+    def col(j):
+        return T.col[:, j:j + 1]
+
+    def C(j):
+        return R("col", j, j + 1)
+
+    def eyes(lst):
+        for name, o, sc in lst:
+            ts(S(name, o, o + 128), S("ahi", 0, 128), col(0), sc, A.is_equal, A.mult, [R("ahi"), C(0)], [R(name, o, o + 128)], 64)
+    iota(T.pi[:, 0:1], [[0, 1]], 0, 1, [R("pi", 0, 1)], 1, small=False)
+    iota(S("ahi"), [[1, 256]], 0, 0, [R("ahi")], 256)
+    iota(S("xg"), [[16, 8], [0, 16]], 0, 0, [R("xg")], 128)
+    iota(S("k1a"), [[16, 16], [0, 16]], 0, 0, [R("k1a")], 256)
+    iota(S("kpa"), [[0, 16], [1, 16]], 0, 0, [R("kpa")], 256)
+    iota(T.con[0:2, :], [[0, 128]], 2040 * 8192, 4096 - 2040 * 8192, [R("con")], 128)
+    iota(T.coo[0:2, :], [[0, 128]], 2040 * 8192, -4096 - 2040 * 8192, [R("coo")], 128)
+    ts(T.pi[:, 1:2], T.pi[:, 0:1], 15, None, A.bitwise_and, None, [R("pi", 0, 1)], [R("pi", 1, 2)], 1)
+    fill("one", 1.0)
+    cp(T.col[:, 0:2], T.pi[:, 0:2], [R("pi")], [R("col", 0, 2)], 2)
+    fill("eb", 0.0, 0, 1)
+    tt(col(2), col(0), col(1), A.subtract, [R("col", 0, 2)], [C(2)], 1)
+    ts(S("alo"), S("ahi"), 0.0, col(1), A.mult, A.add, [R("ahi"), C(1)], [R("alo")], 128)
+    ts(col(5), col(2), 15.0, None, A.add, None, [C(2)], [C(5)], 1)
+    for k in range(2):
+        ts(col(6 + 3 * k), col(1), 2.0 * k, 16.0, A.is_equal, A.mult, [C(1)], [C(6 + 3 * k)], 1)
+        ts(col(7 + 3 * k), col(1), 2.0 * k + 1, None, A.is_equal, None, [C(1)], [C(7 + 3 * k)], 1)
+    for k in range(2):
+        tt(col(8 + 3 * k), col(6 + 3 * k), col(7 + 3 * k), A.add, [R("col", 6 + 3 * k, 8 + 3 * k)], [C(8 + 3 * k)], 1)
+    eyes((("e1", 0, 1.0), ("en1", 0, -1.0), ("e16", 0, 16.0), ("en16", 0, -16.0), ("e256", 0, 256.0)))
+    for name, o, sc in (("gp", 0, 8192.0), ("gn", 0, -8192.0), ("sxy", 0, col(8)), ("sxy", 8, col(11))):
+        ts(S(name, o, o + 8), S("xg", 0, 128, 16), col(2), sc, A.is_equal, A.mult, [R("xg"), R("col")], [R(name, o, o + 8)], 8)
+    fill("fi", 0.0, cyc=256)
+    fill("c256", 256.0, cyc=136)
+    cp(S("cu"), S("ci"), [R("ci")], [R("cu")], 1024)
+    cp(S("chi"), S("ci"), [R("ci")], [R("chi")], 1024)
+    tt(S("clo"), S("ci"), S("chi"), A.subtract, [R("ci"), R("chi")], [R("clo")], 2048)
+
+    def late_constants():
+        eyes((("en1", 128, -1.0), ("en16", 128, -16.0), ("e17", 0, 17.0), ("e272", 0, 272.0)))
+        for name, sc in (("s1w", col(8)), ("s3w", 1.0), ("s4w", 16.0)):
+            ts(S(name), S("ahi", 0, 144), col(5), sc, A.is_equal, A.mult, [R("ahi"), R("col")], [R(name)], 72)
+        ts(S("bd"), S("xg"), col(2), None, A.is_equal, None, [R("xg"), C(2)], [R("bd")], 64)
+        ts(S("nbd"), S("xg"), col(2), -1.0, A.is_equal, A.mult, [R("xg"), C(2)], [R("nbd")], 64)
+        ts(S("ge"), S("ahi", 0, 128), col(0), None, A.is_ge, None, [R("ahi"), C(0)], [R("ge")], 64)
+        ts(S("l1"), S("alo", 0, 16), 17.0, 17.0, A.mult, A.add, [R("alo")], [R("l1")], 16)
+        tt(S("tri"), S("bd"), S("ge"), A.mult, [R("bd"), R("ge")], [R("tri")], 256)
+        ts(S("k1"), S("k1a"), col(1), None, A.add, None, [R("k1a"), C(1)], [R("k1")], 128)
+        ts(S("ntri"), S("tri"), -1.0, None, A.mult, None, [R("tri")], [R("ntri")], 64)
+        ts(S("kp"), S("kpa"), 1.0, None, A.min, None, [R("kpa")], [R("kp")], 128)
+
+    KW, KO, K0, K1, K2, K3 = 2048, (2048, 2560), 2560, 3584, 3072, (2304, 3840)
+    flip = [0]
+
+    def short(src, dst, a, b):
+        d = flip[0] * 1024
+        flip[0] ^= 1
+        mms = []
+        for o, e in blocks(a, b, 512):
+            out = ps[:, d + o - a:d + e - a]
+            mms.append((out, S("e1"), S("w", o, e), True, False, e - o))
+            mms.append((out, S("en1", 0, 128), S(src, o, e), False, True, e - o))
+        pe(mms, [R("e1"), R("en1", 0, 128), R("w", a, b), R(src, a, b)], [P(d, b - a)], 0)
+        ac(S(dst, a, b), ps[:, d:d + b - a], AF.Relu, [P(d, b - a)], [R(dst, a, b)], b - a)
+
+    def sums(k, h, buf, sel, alone=False, n=8):
+        return [(ps[:, k + r:k + 16 * n:16], S(buf, h * 2048 + r, h * 2048 + 2048, 16), S(sel), alone, alone or r == 15, n)
+                for r in range(16)]
+
+    def key(k, h, buf, is_min, d, more=(), prio=1, split=False):
+        out = ps[:, k:k + 128]
+        n = 1 if d == 0 else 2
+        sign = "gn" if is_min else "gp"
+        mms = [(out, T.one[0:n, :], T["coo" if d is None else "con"][0:n, :], True, False, 128)]
+        rd = [R("one"), R("con"), R("coo"), R("e1")] + list(more)
+        a = h * 128
+        if not is_min:
+            mms.append((out, S("en1", 0, 128), S("whi", a, a + 128), False, False, 128))
+            mms.append((out, S("en1", 0, 128), S("wlo", a, a + 128), False, False, 128))
+            rd += [R("en1", 0, 128), R("whi"), R("wlo")]
+        if d is None:
+            mms.append((out, S("ahi", a, a + 128), S("e16"), False, False, 128))
+            mms.append((out, S("alo", a, a + 128), S("e1"), False, False, 128))
+            rd += [R("ahi"), R("alo"), R("e16")]
+        else:
+            a += d * 256
+            mms.append((out, S("chi", a, a + 128), S("e1"), False, False, 128))
+            mms.append((out, S("clo", a, a + 128), S("e1"), False, False, 128))
+            rd += [R("chi"), R("clo")]
+        if split:
+            pe(mms, rd, [P(k, 128)], prio)
+            mms, rd = [], []
+        pe(mms + sums(k, h, buf, sign), rd + [R(buf, h * 2048, h * 2048 + 2048), R(sign)], [P(k, 128)], prio)
+
+    def wrap(k, src, a, b, sel, first, last):
+        n = (b - a) // 16
+        return [(ps[:, k:k + n], S(sel, 15 - r, 143 - r), S(src, a + r, b, 16), first and r == 0, last and r == 15, n)
+                for r in range(16)]
+
+    hcore = helpers(T, topo)[core]
+    for t in range(2):
+        z, zn, xo, x2 = "z%d" % t, "z%d" % (t + 1), "xo%d" % t, "x2%d" % t
+        ZW = R(z, 0, V)
+
+        def vmin(d, dst, a, b):
+            tt(S(dst, a, b), ind(z, V, "cu", d * V + a, d * V + b), S("w", a, b), A.min,
+               [ZW, R("cu"), R("w", a, b)], [R(dst, a, b)], (b - a) * GA)
+
+        def sgather(d, dst, a, b):
+            ac(S(dst, a, b), ind(z, V, "cu", d * V + a, d * V + b), AF.Copy, [ZW, R("cu")], [R(dst, a, b)], (b - a) * GA)
+
+        def merge(src, k, a, b):
+            tt(S("bi", a, b), S(src, a, b), ps[:, k:k + b - a], A.min, [R(src, a, b), P(k, b - a)], [R("bi", a, b)], b - a)
+
+        def clear(a=0, b=256):
+            ts(S("bj", a, b), S("bi", a, b), -4097, None, A.bitwise_and, None, [R("bi", a, b)], [R("bj", a, b)], b - a)
+
+        def parts(h):
+            a, b = h * 128, h * 128 + 128
+            merge("bj", K3[h], a, b)
+            clear(a, b)
+            merge("bj", KO[h], a, b)
+            ts(S("hli", 2 * a, 2 * a + 128), S("bi", a, b), 4, 255, A.arith_shift_right, A.bitwise_and,
+               [R("bi", a, b)], [R("hli", 2 * a, 2 * a + 128)], 128)
+            ts(S("hli", 2 * a + 128, 2 * b), S("bi", a, b), 15, None, A.bitwise_and, None,
+               [R("bi", a, b)], [R("hli", 2 * a + 128, 2 * b)], 128)
+            cp(S("hl", 2 * a, 2 * b), S("hli", 2 * a, 2 * b), [R("hli", 2 * a, 2 * b)], [R("hl", 2 * a, 2 * b)], 256)
+
+        mine = "o0" not in FOLDS[t]
+        far = "g0" in FOLDS[t]
+        pre = PRE if t == 0 else 0
+        if pre:
+            cp(S("zg3", V - pre, V), ind(z, V, "cu", 4 * V - pre, 4 * V), [ZW, R("cu")], [R("zg3", V - pre, V)], pre * GA)
+        for a, b in (wb if t == 0 else blocks(0, V)):
+            vmin(0, "x0", a, b)
+        sgather(2, "zg2", 0, 1024)
+        sgather(2, "zg2", 1024, 2048)
+        eng = topo.engines(core, hcore)
+        for f in FOLDS[t]:
+            dst, a, b = folded(f, t)
+            src = z if f[0] == "o" else "zg2"
+
+            def fold(g, name=f + str(t), a=a, b=b, src=src, dst=dst, eng=eng):
+                rid, pid, _ = topo.addr(hcore)
+                g.remote_dma_fused([RemoteDMATransfer(dst_ids=[DstId(rid=rid, pnc=pid)], dma_engine_mask=sum(1 << e for e in eng),
+                                                      remote_sem=T.sem["out" + name], srcs=[S(src, a, b), S("w", a, b)],
+                                                      dsts=[S(dst, a, b)], alu_op=3)], local_sem=T.sem["sent"])
+                return None
+            add("pool", fold, [R(src, a, b), R("w", a, b), R("w", 2048, 3072)], [R("net" + f + str(t))], 0.5, sem="sent",
+                lat=1.3, inc=len(eng))
+            add("net", None, [R("net" + f + str(t))], [R(dst, a, b)], 3.0, sem="back" + f + str(t), inc=len(topo.engines(hcore, core)))
+        if not far:
+            short("zg2", x2, 0, 1024)
+        if mine:
+            short(z, xo, 0, 1024)
+        sgather(2, "zg2", 2048, 3072)
+        if t == 0:
+            for h in range(2):
+                pe(sums(KW + h * 128, h, "w", "gp", True), [R("w", h * 2048, h * 2048 + 2048), R("gp")], [P(KW + h * 128, 128)], 0)
+            ac(S("whi"), ps[:, KW:KW + 256], AF.Copy, [P(KW, 256)], [R("whi")], 256)
+            tt(S("wlo"), ps[:, KW:KW + 256], S("whi"), A.subtract, [P(KW, 256), R("whi")], [R("wlo")], 256)
+        if not far:
+            short("zg2", x2, 1024, 2048)
+        if mine:
+            short(z, xo, 1024, 2048)
+        for a, b in blocks(0, V):
+            vmin(1, "x1", a, b)
+        for h in range(2):
+            key(K0 + h * 128, h, "x0", True, 0)
+        sgather(2, "zg2", 3072, V)
+        if far:
+            short("zg2", x2, 2048, 3072)
+        ac(S("b0"), ps[:, K0:K0 + 256], AF.Copy, [P(K0, 256)], [R("b0")], 256)
+        dma("sp", "da%d" % t, T.x0[2:128:16, :], S("ahi"), [R("ahi"), R("b0"), R("x0")], [R("t1a")], 64e3)
+        dma("sp", "db%d" % t, T.x0[3:128:16, :], S("alo"), [R("alo"), R("b0"), R("x0")], [R("t1b")], 64e3)
+        if not far:
+            short("zg2", x2, 2048, 3072)
+        sgather(3, "zg3", 2048, 3072)
+        short("zg2", x2, 3072, V)
+        for h in range(2):
+            key(K2 + h * 128, h, x2, far and h == 0, 2, more=[R("x1", 1024, 2048)] if far else [])
+            key(K1 + h * 128, h, "x1", True, 1, prio=-1)
+        sgather(3, "zg3", 3072, V - pre)
+        short("zg3", "x3", 2048, 3072)
+        short("zg3", "x3", 3072, V)
+        vmin(3, "x3", 0, CUTS[0])
+        merge("b0", K1, 0, 256)
+        vmin(3, "x3", CUTS[0], CUTS[1])
+        clear()
+        merge("bj", K2, 0, 256)
+        vmin(3, "x3", CUTS[1], 2048)
+        clear()
+        key(KO[1], 1, xo, True, None, more=[R("x1", 2048, 3072)])
+        key(KO[0], 0, xo, not mine, None, more=[] if mine else [R("x1")])
+        key(K3[1], 1, "x3", False, 3, split=True)
+        key(K3[0], 0, "x3", True, 3, more=[P(KO[0], 128)], split=True)
+        n0 = len(ops)
+        parts(1)
+        n1 = len(ops)
+        parts(0)
+        one, two = ops[n0:n1], ops[n1:]
+        ops[n0:] = [o for pair in zip(one, two) for o in pair]
+
+        def turn(k, terms, own=False):
+            mms = []
+            for h in range(2):
+                out = ps[:, k + h * 128:k + h * 128 + 128]
+                lst = [(S("hl", h * 256 + p * 128, h * 256 + p * 128 + 128), S(e, 0, 128)) for p, e in terms]
+                if own:
+                    lst += [(S("e16"), S("ahi", h * 128, h * 128 + 128)), (S("e1"), S("alo", h * 128, h * 128 + 128))]
+                for i, (l, r_) in enumerate(lst):
+                    mms.append((out, l, r_, i == 0, i == len(lst) - 1, 128))
+            pe(mms, [R("hl"), R("e1"), R("e16"), R("ahi"), R("alo")] + [R(e, 0, 128) for p, e in terms], [P(k, 256)])
+        turn(0, [(0, "e1")])
+        turn(1024, [(1, "e1")])
+        turn(512, [(0, "e1"), (1, "e256")])
+        turn(1536, [(0, "en16"), (1, "en1")], own=True)
+        turn(1792, [(0, "e16"), (1, "e1")])
+        ac(S("fh"), ps[:, 0:256], AF.Copy, [P(0, 256)], [R("fh")], 256)
+        cp(S("fl"), ps[:, 1024:1280], [P(1024, 256)], [R("fl")], 256)
+        dma("act", "dh%d" % t, T.x0[0:128:16, :], S("fh"), [R("fh"), R("x0")], [R("t1h")], 64e3)
+        dma("sp", "dl%d" % t, T.x0[1:128:16, :], S("fl"), [R("fl"), R("x0")], [R("t1l")], 64e3)
+        cp(S("lf"), ps[:, 512:768], [P(512, 256)], [R("lf")], 256)
+        ac(S("di", 0, 512, 2), ps[:, 1536:1792], AF.Copy, [P(1536, 256)], [R("di")], 256)
+        ac(S("di", 1, 512, 2), ps[:, 1792:2048], AF.Copy, [P(1792, 256)], [R("di")], 256)
+        if t == 0:
+            late_constants()
+
+        XY = (3072, 3584)
+        for h in range(2):
+            pe([(ps[:, XY[h]:XY[h] + 256], S("ahi", h * 128, h * 128 + 128), S("en16"), True, False, 256),
+                (ps[:, XY[h]:XY[h] + 256], S("alo", h * 128, h * 128 + 128), S("en1"), False, False, 256)],
+               [R("ahi"), R("alo"), R("en1"), R("en16"), R("hl")], [P(XY[h], 256)])
+
+        def both(win, wres, lst, dst, q, n=512):
+            a, m, b = q * 1024, q * 1024 + n, q * 1024 + 1024
+            cp(S(dst, a, m), ind(win, V, lst, a, m), wres + [R(lst, a // 16, m // 16)], [R(dst, a, m)], n * GA)
+            ac(S(dst, m, b), ind(win, V, lst, m, b), AF.Copy, wres + [R(lst, m // 16, b // 16)], [R(dst, m, b)], (1024 - n) * GA)
+        for q in range(4):
+            both("x0", [R("x0"), R("t1h"), R("t1l"), R("t1a"), R("t1b")], "lf", "t2", q)
+            k = 2048 + q * 64 if q < 3 else 2560
+            pe(wrap(k, "t2", q * 1024, q * 1024 + 1024, "s1w", True, True), [R("t2", q * 1024, q * 1024 + 1024), R("s1w")], [P(k, 64)])
+        cp(S("lg", 0, 192), ps[:, 2048:2240], [P(2048, 192)], [R("lg", 0, 192)], 192)
+        both("t2", [R("t2")], "lg", "t3", 0, G2[0])
+        cp(S("lg", 192, 256), ps[:, 2560:2624], [P(2560, 64)], [R("lg", 192, 256)], 64)
+        both("t2", [R("t2")], "lg", "t3", 1, G2[1])
+        for h in range(2):
+            a, k = h * 128, K3[h]
+            both("t2", [R("t2")], "lg", "t3", 2 + h, G2[2 + h])
+            pe(sums(XY[h], h, "t3", "sxy", n=16), [R("t3", h * 2048, h * 2048 + 2048), R("sxy")], [P(XY[h], 256)])
+            ts(S("nn", 2 * a, 2 * a + 256), ps[:, XY[h]:XY[h] + 256], 0.0, None, A.not_equal, None,
+               [P(XY[h], 256)], [R("nn", 2 * a, 2 * a + 256)], 256)
+            if h:
+                cp(S("fi", 1, 256, 2), ps[:, K3[0]:K3[0] + 128], [P(K3[0], 128)], [R("fi", 0, 256)], 128)
+            tt(S("ft", a, a + 128), S("nn", 2 * a, 2 * a + 128), S("nn", 2 * a + 128, 2 * a + 256), A.mult,
+               [R("nn", 2 * a, 2 * a + 256)], [R("ft", a, a + 128)], 256)
+            pe([(ps[:, k:k + 128], S("ft", a, a + 128), S("e1"), True, True, 128)], [R("ft", a, a + 128), R("e1")], [P(k, 128)])
+        ac(S("fi", 257, 512, 2), ps[:, K3[1]:K3[1] + 128], AF.Copy, [P(K3[1], 128)], [R("fi", 256, 512)], 128)
+        for k, m, nm in ((0, "bd", "nbd"), (1024, "tri", "ntri")):
+            pe([(ps[:, k + 256:k + 272], S(m), S("one", 0, 16), True, False, 16),
+                (ps[:, k + 256:k + 272], S(nm), S("fi", 1, 32, 2), False, True, 16),
+                (ps[:, k:k + 128], S(m), S("fi", 1, 256, 2), True, True, 128)],
+               [R("fi", 0, 256), R(m), R(nm), R("one")], [P(k, 272)])
+        for k, m in ((128, "bd"), (1152, "tri")):
+            pe([(ps[:, k:k + 128], S(m), S("fi", 257, 512, 2), True, True, 128)], [R("fi", 256, 512), R(m)], [P(k, 128)])
+        scan(S("pp"), S("fi"), S("di"), A.mult, A.add, [R("fi"), R("di")], [R("pp")], 512)
+        scan(S("eb", 1, 273), ps[:, 0:272], S("c256"), A.add, A.min, [P(0, 272), R("c256")], [R("eb", 1, 273)], 272)
+        pe([(ps[:, 512:528], S("s3w", 15 - r, 143 - r), S("eb", 1 + r, 1 + r + 256, 17), r == 0, r == 15, 16) for r in range(16)],
+           [R("eb"), R("s3w")], [P(512, 16)])
+        ac(S("tb"), ps[:, 512:528], AF.Copy, [P(512, 16)], [R("tb")], 16, scale=0.0625)
+        tt(S("m1"), ind("eb", 273, "l1", 0, 256), S("k1"), A.is_le, [R("eb"), R("l1"), R("k1")], [R("m1")], 256 * GA)
+        scan(S("s1"), S("kp"), S("m1"), A.mult, A.add, [R("kp"), R("m1")], [R("s1")], 128)
+        cp(S("l2"), S("s1", 15, 256, 16), [R("s1")], [R("l2")], 16)
+        tt(S("m2"), ind("tb", 16, "l2", 0, 256), S("ahi"), A.is_le, [R("tb"), R("l2"), R("ahi")], [R("m2")], 256 * GA)
+        pe([(ps[:, 3072:3088], S("e17"), S("s1", 15, 256, 16), True, False, 16)] + wrap(3072, "m2", 0, 256, "s3w", False, True),
+           [R("s1"), R("m2"), R("e17"), R("s3w")], [P(3072, 16)])
+        pe([(ps[:, 3584:3600], S("e272"), S("s1", 15, 256, 16), True, False, 16)] + wrap(3584, "m2", 0, 256, "s4w", False, False),
+           [R("s1"), R("m2"), R("e272"), R("s4w")], [P(3584, 16)])
+        cp(S("lp"), S("pp", 1, 512, 2), [R("pp")], [R("lp")], 256)
+        tt(S("pin"), S("eb", 0, 272), ps[:, 1024:1296], A.add, [R("eb"), P(1024, 272)], [R("pin")], 272)
+        cp(S("l3"), ps[:, 3072:3088], [P(3072, 16)], [R("l3")], 16)
+        tt(S("m3"), ind("pin", 272, "l3", 0, 256), S("ahi"), A.is_le, [R("pin"), R("l3"), R("ahi")], [R("m3")], 256 * GA)
+        pe(wrap(3584, "m3", 0, 256, "s3w", False, True), [R("m3"), R("s3w")], [P(3584, 16)])
+        cp(S(z, V, V + 256), ind(z, V, "lp", 0, 256), [ZW, R("lp")], [R(z, V, V + 256)], 256 * GA)
+        cp(S("lv"), ps[:, 3584:3600], [P(3584, 16)], [R("lv")], 16)
+        away, land = "away%d" % t, "land%d" % t
+        cp(S(away), ind(z, V + 256, "lv", 0, 256), [R(z), R("lv")], [R(away)], 256 * GA)
+        dst = T.cores[(rank + 1 + t) % n_ranks]
+        eng = topo.engines(core, dst)
+        got = len(topo.engines(T.cores[(rank - 1 - t) % n_ranks], core))
+
+        def send(g, t=t, dst=dst, eng=eng, away=away, land=land):
+            rid, pid, _ = topo.addr(dst)
+            g.remote_dma(S(land), S(away), T.sem["arr%d" % t], T.sem["sent"], pid, rid, sum(1 << e for e in eng))
+            return None
+        add("pool", send, [R(away)], [R("net%d" % t)], 0.3, sem="sent", lat=0.3, inc=len(eng))
+        add("net", None, [R("net%d" % t)], [R(land)], 0.0, sem="arr%d" % t, inc=got)
+        for a, b in blocks(0, ZS):
+            ac(S(zn, a, b), ind(z, V, "lp", a, b), AF.Copy, [ZW, R("lp")], [R(zn, a, b)], (b - a) * GA)
+        cp(S("oi"), ps[:, 3584:3600], [P(3584, 16)], [R("oi")], 16)
+        cp(S(zn, ZS, V - 512), ind(z, V, "lp", ZS, V - 512), [ZW, R("lp")], [R(zn, ZS, V - 512)], (V - 512 - ZS) * GA)
+        ts(S("oj"), S("oi"), 4095, None, A.bitwise_and, None, [R("oi")], [R("oj")], 16)
+        cp(S(zn, V - 512, V), ind(z, V, "lp", V - 512, V), [ZW, R("lp")], [R(zn, V - 512, V)], 512 * GA)
+        cp(S("lo"), S("oj"), [R("oj")], [R("lo")], 16)
+        cp(ind(zn, V, "lo", 0, 256), S(land), [R(land), R("lo")], [R(zn, 0, V)], 256 * SC)
+    dma("sp", "dy0", T.y[:, 0:2048], S("z2", 0, 2048), [R("z2")], [R("y", 0, 1)], 512e3)
+    dma("act", "dy1", T.y[:, 2048:V], S("z2", 2048, V), [R("z2")], [R("y", 1, 2)], 512e3)
+    return ops
+
+
+def _meet(x, y):
+    return x[0] == y[0] and x[1] < y[2] and y[1] < x[2]
+
+
+def _banks(o):
+    s = set()
+    for r in o["rd"] + o["wr"]:
+        if r[0] == "ps":
+            s.update(range(r[1] // 512, (r[2] - 1) // 512 + 1))
+    return s
+
+
+def order(ops):
+    n = len(ops)
+    banks = [_banks(o) for o in ops]
+    deps = [[] for _ in ops]
+    prev = [None] * n
+    last = {}
+    for j in range(n):
+        b = ops[j]
+        if b["q"] not in ("pe", "net"):
+            prev[j] = last.get(b["q"])
+            last[b["q"]] = j
+        for i in range(j):
+            a = ops[i]
+            if (any(_meet(x, y) for x in a["wr"] for y in b["rd"] + b["wr"]) or any(_meet(x, y) for x in a["rd"] for y in b["wr"])
+                    or (a["q"] != b["q"] and banks[i] & banks[j])):
+                deps[j].append(i)
+    done = [None] * n
+    free = {}
+    ring = 0.0
+    seq = []
+    left = list(range(n))
+    while left:
+        best = None
+        for j in left:
+            if (prev[j] is not None and done[prev[j]] is None) or any(done[i] is None for i in deps[j]):
+                continue
+            st = max([free.get(ops[j]["q"], 0.0)] + [done[i] + WAKE for i in deps[j]])
+            k = (round(st / 0.2), ops[j]["prio"], j)
+            if best is None or k < best[0]:
+                best = (k, j, st)
+        _, j, st = best
+        o = ops[j]
+        if o["q"] != "net":
+            free[o["q"]] = st + o["cost"]
+        if o["sem"] and o["q"] != "net":
+            ring = max(ring, st + DLAT) + o["lat"]
+            done[j] = ring
+        else:
+            done[j] = st + o["cost"]
+        left.remove(j)
+        seq.append(j)
+    return seq, deps
+
+
+def hand_back(g, core, home, T, topo):
+    rid, pid, _ = topo.addr(home)
+    eng = topo.engines(core, home)
+    for t in range(2):
+        for f in FOLDS[t]:
+            buf, a, b = folded(f, t)
+            g.wait_ge(T.sem["out" + f + str(t)], len(topo.engines(home, core)))
+            g.remote_dma(T[buf][:, a:b], T[buf][:, a:b], T.sem["back" + f + str(t)], T.sem["sent"], pid, rid, sum(1 << e for e in eng))
+    g.wait_ge(T.sem["sent"], sum(len(f) for f in FOLDS) * len(eng))
+
+
+def rank_program(g, core, T, topo):
+    if T.rank_of(core) is None:
+        for home, h in helpers(T, topo).items():
+            if h == core:
+                hand_back(g, core, home, T, topo)
+        return
+    ops = plan(T, topo, core)
+    seq, deps = order(ops)
+    queue = {"pe": g.tensor, "dve": g.vector, "act": g.scalar, "pool": g, "sp": g.sync}
+    place = {j: k for k, j in enumerate(seq)}
+    seen = {q: {} for q in list(queue) + ["net"]}
+    after = {}
+    waits = {}
+    for j in seq:
+        o = ops[j]
+        know = seen[o["q"]]
+        need = []
+        for i in sorted(deps[j], key=lambda i: -place[i]):
+            a = ops[i]
+            if o["q"] == "net" or (a["q"] == "pe" and o["q"] == "pe"):
+                continue
+            if know.get(a["sem"] or a["q"], -1) >= place[i]:
+                continue
+            need.append(i)
+            for k, v in after[i].items():
+                know[k] = max(know.get(k, -1), v)
+        waits[j] = need
+        after[j] = {} if o["q"] == "net" else dict(know)
+        after[j][o["sem"] or o["q"]] = place[j]
+    marked = set(i for j in seq for i in waits[j])
+    count = {}
+    value = {}
+    for j in seq:
+        o = ops[j]
+        if o["sem"] or j in marked:
+            s = o["sem"] or o["q"]
+            count[s] = count.get(s, 0) + (o["inc"] if o["sem"] else 1)
+            value[j] = (s, count[s])
+    for j in seq:
+        o = ops[j]
+        if o["q"] == "net":
+            continue
+        for i in waits[j]:
+            queue[o["q"]].wait_ge(T.sem[value[i][0]], value[i][1])
+        ins = o["fn"](g)
+        if j in value and ins is not None:
+            ins.then_inc(T.sem[value[j][0]], 16 if o["sem"] else 1)
+    for s in sorted(count, key=lambda s: s.startswith("dy")):
+        g.wait_ge(T.sem[s], count[s])

@@ -2,31 +2,40 @@ from concourse.bass import DstId, RemoteDMATransfer
 from concourse.mybir import AluOpType as A, ActivationFunctionType as AF
 
 V = 4096
-FOLDS = (("o2", "o3", "o0", "o1"), ("o2", "o3", "o0", "o1"))
-PRE = 0
-WB = (0, 512, 1024, 2048, 3072, V)
-CUTS = (1280, 1792)
-G2 = (512, 512, 448, 320)
-ZS = 2944
+LOADS = (("z0", 0, 768, 0), ("w", 0, 768, 0), ("ci", 0, 1024, 0), ("z0", 768, V, 0), ("w", 768, 2048, 0), ("w", 2048, V, 0))
+VO = 512
+FOLDS = (((4, VO, 768), (4, 768, 2048), (4, 2048, 3072), (4, 3072, V)),
+         ((4, 0, 1024), (4, 1024, 2048), (4, 2048, 3072), (4, 3072, V)))
+G1 = (512, 512, 512, 480)
+G2 = (992, 512, 416)
+ZS = 3328
+BASE = 2040 * 8192
 
-BF, F32, I32, U16 = "bfloat16", "float32", "int32", "uint16"
+BF, F16, F32, I32, U16 = "bfloat16", "float16", "float32", "int32", "uint16"
 SCRATCH = {"ps": ("psum", [128, 4096], F32)}
 for _dt, _names in (
-        (BF, "z0:4352 z1:4352 z2:4096 w:4096 chi:1024 clo:1024 x0:4096 x1:4096 x3:4096 x20:4096 x21:4096 xo0:4096 xo1:4096 "
-             "zg2:4096 zg3:4096 t2:4096 t3:4096 whi:256 wlo:256 hl:512 fh:256 fl:256 fi:512 nn:512 ft:256 eb:288 pin:272 "
+        (BF, "z0:4352 z1:4352 z2:4096 w:4096 x00:4096 x01:4096 x10:4096 x20:4096 x21:4096 x30:4096 x31:4096 x40:4096 x41:4096 "
+             "zg2:4096 zg3:4096 t2:4096 t3:4096 whi:256 wlo:256 hl:512 fi:512 nn:512 eb:288 pin:272 "
              "c256:272 tb:16 m1:256 s1:256 m2:256 m3:256 away0:256 away1:256 land0:256 land1:256 ahi:256 alo:256 k1:256 "
-             "k1a:256 kp:256 kpa:256 xg:128 con:128 coo:128 one:128 e1:128 en1:256 e16:128 en16:256 e256:128 e17:128 "
-             "e272:128 bd:128 nbd:128 ge:128 tri:128 ntri:128 gp:8 gn:8 sxy:16 s1w:144 s3w:144 s4w:144"),
-        (F32, "b0:256 di:512 pp:512 col:16"),
-        (I32, "ci:1024 bi:256 bj:256 hli:512 oi:16 oj:16 pi:2"),
+             "k1a:256 kp:256 xg:128 con:384 ht:256 one:256 e1:128 en1:256 e16:128 en16:256 e256:128 e17:128 "
+             "e272:128 bd:128 nbd:128 tri:128 ntri:128 gp:8 gn:8 sxy:16 s1w:144 s3w:144 s4w:144 skp:144 skn:144"),
+        (F16, "c16:1280 eh:128"),
+        (F32, "b0:256 pf:256 di:512 pp:512 col:16 ef:128"),
+        (I32, "ci:1024 bi:256 bj:256 hli:512 hti:256 oi:16 oj:16 pi:2"),
         (U16, "cu:1024 lf:256 lg:256 lp:256 l1:16 l2:16 l3:16 lv:16 lo:16")):
     for _x in _names.split():
         SCRATCH[_x.split(":")[0]] = ("sbuf", [128, int(_x.split(":")[1])], _dt)
-SEMAPHORES = (["pe", "dve", "act", "pool", "arr0", "arr1", "sent", "dc", "dz", "da0", "db0", "da1", "db1",
-               "dh0", "dl0", "dh1", "dl1", "dy0", "dy1"] + ["dw%d" % q for q in range(len(WB) - 1)]
-              + [p + f + str(t) for p in ("out", "back") for t in range(2) for f in FOLDS[t]])
+SEMAPHORES = (["pe", "dve", "act", "pool", "arr0", "arr1", "sent", "da", "db", "dh0", "dl0", "dh1", "dl1", "dy0", "dy1"]
+              + ["d%s%d" % x[:2] for x in LOADS]
+              + ["%s%d%d" % (p, t, q) for p in ("left", "out", "back") for t in range(2) for q in range(len(FOLDS[t]))])
 
-CY, GA, SC, PC, WAKE, DLAT, DRATE = 0.00095, 1.55, 3.5, 0.00048, 0.12, 2.0, 200e3
+CY, GA, SC, PC, VFIX, SFIX, AFIX, AR, WAKE = 0.00086, 1.45, 3.5, 0.00042, 0.06, 0.08, 0.08, 1.1, 0.07
+DLAT, RLAT, DRATE, ROWS, FOLD, AHEAD = 0.8, 1.6, 400e3, 0.2, 2.5, 0.4
+LOOSE, PASSES = ("pe", "net"), 0
+
+
+def mins(d, t):
+    return "x%d%d" % (d, 0 if d == 1 else t)
 
 
 def helpers(T, topo):
@@ -38,393 +47,429 @@ def helpers(T, topo):
     return out
 
 
-def folded(f, t):
-    return ("xo%d" if f[0] == "o" else "x2%d") % t, int(f[1]) * 1024, int(f[1]) * 1024 + 1024
+def S(name, a=0, b=None, s=1, p=(0, 128, 1)):
+    return (name, a, SCRATCH[name][1][1] if b is None else b, s) + p
+
+
+def P(a, n, s=1):
+    return S("ps", a, a + n, s)
+
+
+def ind(win, n, lst, a, b):
+    return ("ind", S(win, 0, n), S(lst, a // 16, b // 16))
+
+
+def width(x):
+    return 16 * width(x[2]) if x[0] == "ind" else len(range(x[1], x[2], x[3]))
+
+
+def narrow(x):
+    return SCRATCH[x[0]][2] in (BF, F16, U16)
+
+
+def blocks(a, b, n=1024):
+    return [(o, min(o + n, b)) for o in range(a, b, n)]
 
 
 def plan(T, topo, core):
     ops = []
     rank = T.rank_of(core)
     n_ranks = len(T.cores)
-    ps = T.ps
 
-    def add(q, fn, rd, wr, cost, sem=None, lat=0.0, inc=16, prio=1):
-        ops.append({"q": q, "fn": fn, "rd": rd, "wr": wr, "cost": cost, "sem": sem, "lat": lat, "inc": inc, "prio": prio})
+    def ap(x):
+        if not isinstance(x, tuple):
+            return x
+        if x[0] == "ind":
+            return ap(x[1]).indirect(ap(x[2]))
+        return T[x[0]][x[4]:x[5]:x[6], x[1]:x[2]:x[3]]
 
-    def R(name, a=0, b=1 << 20):
-        return (name, a, b)
+    def add(q, fn, rd, wr, cost, sem=None, lat=0.0, inc=16, part=False):
+        reads, writes = [], []
+        for x in rd:
+            if isinstance(x, tuple):
+                reads += [x[1], x[2]] if x[0] == "ind" else [x]
+        for x in wr:
+            if x[0] == "ind":
+                reads.append(x[2])
+                x = x[1]
+            writes.append(x)
+        ops.append({"q": q, "fn": fn, "rd": reads, "wr": writes, "cost": cost, "sem": sem, "lat": lat, "inc": inc, "part": part})
 
-    def P(a, n):
-        return ("ps", a, a + n)
+    def took(out, in_, plain, fix=VFIX):
+        if "ind" in (out[0], in_[0]):
+            return fix + CY * width(out) * (SC if out[0] == "ind" else GA)
+        return CY * max(64, width(out) * plain)
 
-    def S(name, a=None, b=None, s=None):
-        return T[name][:, a:b:s]
+    def fast(*xs):
+        return 0.5 if all(x[0] != "ind" and narrow(x) for x in xs) else 1
 
-    def dve(fn, rd, wr, cyc):
-        add("dve", fn, rd, wr, 0.06 + max(cyc, 64) * CY)
+    def ts(out, in0, s1, s2, op0, op1=None):
+        args = (ap(out), ap(in0), ap(s1), ap(s2), op0) + (() if op1 is None else (op1,))
+        add("dve", lambda g: g.vector.tensor_scalar(*args), [in0, s1, s2], [out], took(out, in0, fast(out, in0)))
 
-    def pe(mms, rd, wr, prio=1):
+    def tt(out, in0, in1, op):
+        add("dve", lambda g: g.vector.tensor_tensor(ap(out), ap(in0), ap(in1), op), [in0, in1], [out],
+            took(out, in0, 1 if "ps" in (in0[0], in1[0]) else 2))
+
+    def cp(out, in_):
+        add("dve", lambda g: g.vector.tensor_copy(ap(out), ap(in_)), [in_], [out], took(out, in_, fast(out, in_)))
+
+    def scan(out, d0, d1, op0, op1, first=0.0):
+        add("dve", lambda g: g.vector.tensor_tensor_scan(ap(out), ap(d0), ap(d1), ap(first), op0, op1), [d0, d1, first], [out],
+            took(out, d0, fast(out, d0, d1)))
+
+    def fill(out, val):
+        add("dve", lambda g: g.vector.memset(ap(out), val), [], [out], took(out, out, fast(out)))
+
+    def ac(out, in_, func=AF.Copy, scale=1.0, bias=None):
+        kw = {"scale": ap(scale)} if bias is None else {"scale": ap(scale), "bias": ap(bias)}
+        add("act", lambda g: g.scalar.activation(ap(out), ap(in_), func, **kw), [in_, scale, bias], [out],
+            took(out, in_, AR, SFIX) + (0 if in_[0] == "ind" else AFIX))
+
+    def iota(out, pat, base, cm):
+        kw = {} if SCRATCH[out[0]][2] == I32 else {"allow_small_or_imprecise_dtypes": True}
+        add("pool", lambda g: g.iota(ap(out), pat, base, cm, **kw), [], [out], 0.13 + 2 * width(out) * CY)
+
+    def keep(out, in_, pat, op, cm):
+        add("pool", lambda g: g.affine_select(ap(out), ap(in_), pat, op, 0.0, 0, cm), [in_], [out], 0.17 + 2 * width(out) * CY)
+
+    def pe(mms, first=True, last=True, prio=1, more=()):
         def fn(g):
-            last = None
-            for m in mms:
-                last = g.tensor.matmul(m[0], m[1], m[2], m[3], m[4])
-            return last
-        add("pe", fn, rd, wr, 0.03 + sum(max(64, m[5]) for m in mms) * PC, prio=prio)
+            ins = None
+            for i, m in enumerate(mms):
+                ins = g.tensor.matmul(ap(m[0]), ap(m[1]), ap(m[2]), first and i == 0, last and i == len(mms) - 1)
+            return ins
+        cost = sum(max(64, width(m[2])) * (1 if narrow(m[1]) else 4) for m in mms) * PC
+        add("pe", fn, list(set(x for m in mms for x in m[1:])) + list(more), list(set(m[0] for m in mms)), cost, part=not (first and last))
 
     def dma(q, sem, out, in_, rd, wr, nbytes):
-        add(q, lambda g: (g.sync if q == "sp" else g.scalar).dma_start(out, in_), rd, wr, 0.05, sem=sem, lat=nbytes / DRATE)
+        add(q, lambda g: (g.sync if q == "sp" else g.scalar).dma_start(out, in_), rd, wr, 0.05, sem=sem, lat=ROWS + nbytes / DRATE)
 
-    def ts(out, in0, s1, s2, op0, op1, rd, wr, cyc):
-        if op1 is None:
-            dve(lambda g: g.vector.tensor_scalar(out, in0, s1, None, op0), rd, wr, cyc)
-        else:
-            dve(lambda g: g.vector.tensor_scalar(out, in0, s1, s2, op0, op1), rd, wr, cyc)
+    def move(q, sem, out, in_):
+        dma(q, sem, ap(out), ap(in_), [in_], [out], 256.0 * width(in_))
 
-    def tt(out, in0, in1, op, rd, wr, cyc):
-        dve(lambda g: g.vector.tensor_tensor(out, in0, in1, op), rd, wr, cyc)
+    hcore = helpers(T, topo)[core]
+    line = []
 
-    def cp(out, in_, rd, wr, cyc):
-        dve(lambda g: g.vector.tensor_copy(out, in_), rd, wr, cyc)
+    def turn_of(after):
+        line.append(("line", len(line), len(line) + 1, 1, 0, 1, 1))
+        return [line[-1 - after]] if after and after < len(line) else [], [line[-1]]
 
-    def scan(out, d0, d1, op0, op1, rd, wr, cyc):
-        dve(lambda g: g.vector.tensor_tensor_scan(out, d0, d1, 0.0, op0, op1), rd, wr, cyc)
+    def load(name, src, a, b, after):
+        rd, wr = turn_of(after)
+        dma("sp", "d%s%d" % (name, a), ap(S(name, a, b)), src[:, a:b], rd, wr + [S(name, a, b)], (256.0, 512.0)[name == "ci"] * (b - a))
 
-    def fill(name, val, a=None, b=None, cyc=64):
-        dve(lambda g: g.vector.memset(S(name, a, b), val), [], [R(name, a or 0, b or 1 << 20)], cyc)
+    def fold(t, q, after):
+        d, a, b = FOLDS[t][q]
+        srcs, dst = (S("z%d" % t if d == 4 else "zg%d" % d, a, b), S("w", a, b)), S(mins(d, t), a, b)
+        eng = topo.engines(core, hcore)
+        rd, wr = turn_of(after)
 
-    def ac(out, in_, func, rd, wr, cyc, scale=1.0):
-        add("act", lambda g: g.scalar.activation(out, in_, func, scale=scale), rd, wr, 0.07 + max(cyc, 64) * CY)
-
-    def iota(out, pat, base, cm, wr, n, small=True):
-        if small:
-            add("pool", lambda g: g.iota(out, pat, base, cm, allow_small_or_imprecise_dtypes=True), [], wr, 0.13 + 2 * n * CY)
-        else:
-            add("pool", lambda g: g.iota(out, pat, base, cm), [], wr, 0.13 + 2 * n * CY)
-
-    def ind(win, n, lst, a, b):
-        return T[win][:, 0:n].indirect(T[lst][:, a // 16:b // 16])
-
-    def blocks(a, b, n=1024):
-        return [(o, min(o + n, b)) for o in range(a, b, n)]
-
-    wb = list(zip(WB[:-1], WB[1:]))
-    dma("sp", "dc", S("ci"), T.cand[:], [], [R("ci")], 512e3)
-    for q, (a, b) in enumerate(wb):
-        dma("sp", "dw%d" % q, S("w", a, b), T.wish[:, a:b], [], [R("w", a, b)], 256.0 * (b - a))
-        if q == 0:
-            dma("sp", "dz", S("z0", 0, V), T.goods[:], [], [R("z0", 0, V)], 1024e3)
+        def fn(g):
+            rid, pid, _ = topo.addr(hcore)
+            g.remote_dma_fused([RemoteDMATransfer(dst_ids=[DstId(rid=rid, pnc=pid)], dma_engine_mask=sum(1 << e for e in eng),
+                                                  remote_sem=T.sem["out%d%d" % (t, q)], srcs=[ap(x) for x in srcs], dsts=[ap(dst)],
+                                                  alu_op=3)], local_sem=T.sem["left%d%d" % (t, q)])
+            return None
+        add("pool", fn, list(srcs) + rd, wr, 0.1, sem="left%d%d" % (t, q), lat=2 * ROWS + (b - a) * 256 * FOLD / DRATE, inc=len(eng))
+        add("net", None, wr, [dst], WAKE + RLAT + ROWS + (b - a) * 256 / DRATE, sem="back%d%d" % (t, q), inc=len(topo.engines(hcore, core)))
+    for name, a, b, after in LOADS:
+        load(name, {"ci": T.cand, "z0": T.goods, "w": T.wish}[name], a, b, after)
 
     def col(j):
-        return T.col[:, j:j + 1]
-
-    def C(j):
-        return R("col", j, j + 1)
-
-    def eyes(lst):
-        for name, o, sc in lst:
-            ts(S(name, o, o + 128), S("ahi", 0, 128), col(0), sc, A.is_equal, A.mult, [R("ahi"), C(0)], [R(name, o, o + 128)], 64)
-    iota(T.pi[:, 0:1], [[0, 1]], 0, 1, [R("pi", 0, 1)], 1, small=False)
-    iota(S("ahi"), [[1, 256]], 0, 0, [R("ahi")], 256)
-    iota(S("xg"), [[16, 8], [0, 16]], 0, 0, [R("xg")], 128)
-    iota(S("k1a"), [[16, 16], [0, 16]], 0, 0, [R("k1a")], 256)
-    iota(S("kpa"), [[0, 16], [1, 16]], 0, 0, [R("kpa")], 256)
-    iota(T.con[0:2, :], [[0, 128]], 2040 * 8192, 4096 - 2040 * 8192, [R("con")], 128)
-    iota(T.coo[0:2, :], [[0, 128]], 2040 * 8192, -4096 - 2040 * 8192, [R("coo")], 128)
-    ts(T.pi[:, 1:2], T.pi[:, 0:1], 15, None, A.bitwise_and, None, [R("pi", 0, 1)], [R("pi", 1, 2)], 1)
-    fill("one", 1.0)
-    cp(T.col[:, 0:2], T.pi[:, 0:2], [R("pi")], [R("col", 0, 2)], 2)
-    fill("eb", 0.0, 0, 1)
-    tt(col(2), col(0), col(1), A.subtract, [R("col", 0, 2)], [C(2)], 1)
-    ts(S("alo"), S("ahi"), 0.0, col(1), A.mult, A.add, [R("ahi"), C(1)], [R("alo")], 128)
-    ts(col(5), col(2), 15.0, None, A.add, None, [C(2)], [C(5)], 1)
+        return S("col", j, j + 1)
+    two = (0, 2, 1)
+    iota(S("pi", 0, 1), [[0, 1]], 0, 1)
+    iota(S("ahi"), [[1, 256]], 0, 0)
+    iota(S("xg"), [[16, 8], [0, 16]], 0, 0)
+    for k in range(3):
+        iota(S("con", 128 * k, 128 * k + 128, p=two), [[0, 128]], BASE, 6144 - 4096 * k - BASE)
+    iota(S("k1a"), [[16, 16], [0, 16]], 0, 0)
+    ts(S("pi", 1, 2), S("pi", 0, 1), 15, None, A.bitwise_and)
+    fill(S("one"), 1.0)
+    cp(S("col", 0, 2), S("pi"))
+    fill(S("c256"), 256.0)
+    tt(col(2), col(0), col(1), A.subtract)
+    fill(S("fi"), 0.0)
+    ts(col(5), col(2), 15.0, None, A.add)
     for k in range(2):
-        ts(col(6 + 3 * k), col(1), 2.0 * k, 16.0, A.is_equal, A.mult, [C(1)], [C(6 + 3 * k)], 1)
-        ts(col(7 + 3 * k), col(1), 2.0 * k + 1, None, A.is_equal, None, [C(1)], [C(7 + 3 * k)], 1)
+        ts(col(6 + 3 * k), col(1), 2.0 * k, 16.0, A.is_equal, A.mult)
+        ts(col(7 + 3 * k), col(1), 2.0 * k + 1, None, A.is_equal)
     for k in range(2):
-        tt(col(8 + 3 * k), col(6 + 3 * k), col(7 + 3 * k), A.add, [R("col", 6 + 3 * k, 8 + 3 * k)], [C(8 + 3 * k)], 1)
-    eyes((("e1", 0, 1.0), ("en1", 0, -1.0), ("e16", 0, 16.0), ("en16", 0, -16.0), ("e256", 0, 256.0)))
-    for name, o, sc in (("gp", 0, 8192.0), ("gn", 0, -8192.0), ("sxy", 0, col(8)), ("sxy", 8, col(11))):
-        ts(S(name, o, o + 8), S("xg", 0, 128, 16), col(2), sc, A.is_equal, A.mult, [R("xg"), R("col")], [R(name, o, o + 8)], 8)
-    fill("fi", 0.0, cyc=256)
-    fill("c256", 256.0, cyc=136)
-    cp(S("cu"), S("ci"), [R("ci")], [R("cu")], 1024)
-    cp(S("chi"), S("ci"), [R("ci")], [R("chi")], 1024)
-    tt(S("clo"), S("ci"), S("chi"), A.subtract, [R("ci"), R("chi")], [R("clo")], 2048)
+        tt(col(8 + 3 * k), col(6 + 3 * k), col(7 + 3 * k), A.add)
+    fill(S("eb", 0, 1), 0.0)
+    ts(S("e1"), S("ahi", 0, 128), col(0), None, A.is_equal)
+    ts(S("eh"), S("ahi", 0, 128), col(0), None, A.is_equal)
+    ts(S("s3w"), S("ahi", 0, 144), col(5), None, A.is_equal)
+    ts(S("bd"), S("xg"), col(2), None, A.is_equal)
+    ts(col(3), col(1), -2048.0, None, A.add)
+    ts(S("l1"), S("ahi", 0, 16), 0.0, col(1), A.mult, A.add)
+    ts(S("c16", 1024), S("ahi"), 16.0, col(3), A.mult, A.add)
+    ts(S("l1"), S("l1"), 17.0, 17.0, A.mult, A.add)
+    keep(S("tri"), S("bd"), [[1, 128]], A.is_ge, -1)
+    fold(0, 0, 0)
+    keep(S("kp"), S("one"), [[0, 16], [1, 16]], A.not_equal, 0)
+    ac(S("alo"), S("ahi"), AF.Identity, 0.0, col(1))
 
-    def late_constants():
-        eyes((("en1", 128, -1.0), ("en16", 128, -16.0), ("e17", 0, 17.0), ("e272", 0, 272.0)))
-        for name, sc in (("s1w", col(8)), ("s3w", 1.0), ("s4w", 16.0)):
-            ts(S(name), S("ahi", 0, 144), col(5), sc, A.is_equal, A.mult, [R("ahi"), R("col")], [R(name)], 72)
-        ts(S("bd"), S("xg"), col(2), None, A.is_equal, None, [R("xg"), C(2)], [R("bd")], 64)
-        ts(S("nbd"), S("xg"), col(2), -1.0, A.is_equal, A.mult, [R("xg"), C(2)], [R("nbd")], 64)
-        ts(S("ge"), S("ahi", 0, 128), col(0), None, A.is_ge, None, [R("ahi"), C(0)], [R("ge")], 64)
-        ts(S("l1"), S("alo", 0, 16), 17.0, 17.0, A.mult, A.add, [R("alo")], [R("l1")], 16)
-        tt(S("tri"), S("bd"), S("ge"), A.mult, [R("bd"), R("ge")], [R("tri")], 256)
-        ts(S("k1"), S("k1a"), col(1), None, A.add, None, [R("k1a"), C(1)], [R("k1")], 128)
-        ts(S("ntri"), S("tri"), -1.0, None, A.mult, None, [R("tri")], [R("ntri")], 64)
-        ts(S("kp"), S("kpa"), 1.0, None, A.min, None, [R("kpa")], [R("kp")], 128)
+    def scaled(lst):
+        for out, src, sc in lst:
+            ac(out, src, AF.Identity if isinstance(sc, tuple) else AF.Copy, sc)
+    scaled(((S("en1", 0, 128), S("e1"), -1.0), (S("gn"), S("bd", s=16), -8192.0), (S("gp"), S("bd", s=16), 8192.0),
+            (S("e16"), S("e1"), 16.0), (S("ef"), S("e1"), 1.0), (S("skp"), S("s3w"), 8192.0), (S("e256"), S("e1"), 256.0),
+            (S("en16", 0, 128), S("e1"), -16.0), (S("en1", 128), S("e1"), -1.0), (S("en16", 128), S("e1"), -16.0),
+            (S("s1w"), S("s3w"), col(8)), (S("sxy", 0, 8), S("bd", s=16), col(8)), (S("sxy", 8), S("bd", s=16), col(11))))
 
-    KW, KO, K0, K1, K2, K3 = 2048, (2048, 2560), 2560, 3584, 3072, (2304, 3840)
+    scaled(((S("nbd"), S("bd"), -1.0), (S("e17"), S("e1"), 17.0), (S("e272"), S("e1"), 272.0), (S("s4w"), S("s3w"), 16.0),
+            (S("ntri"), S("tri"), -1.0)))
+    ac(S("k1"), S("k1a"), AF.Identity, 1.0, col(1))
+
+    if VO:
+        tt(S("x40", 0, VO), S("z0", 0, VO), S("w", 0, VO), A.min)
+    cp(S("cu"), S("ci"))
+    ts(S("c16", 0, 1024), S("ci"), -2048.0, None, A.add)
+
+    KEY = ((2048, 2176), (2560, 3072), (2688, 2816), (2048, 3200), (3712, 2432))
+    KP, KF, KW, KT = 3968, 2560, 3584, 2176
     flip = [0]
 
     def short(src, dst, a, b):
         d = flip[0] * 1024
         flip[0] ^= 1
-        mms = []
         for o, e in blocks(a, b, 512):
-            out = ps[:, d + o - a:d + e - a]
-            mms.append((out, S("e1"), S("w", o, e), True, False, e - o))
-            mms.append((out, S("en1", 0, 128), S(src, o, e), False, True, e - o))
-        pe(mms, [R("e1"), R("en1", 0, 128), R("w", a, b), R(src, a, b)], [P(d, b - a)], 0)
-        ac(S(dst, a, b), ps[:, d:d + b - a], AF.Relu, [P(d, b - a)], [R(dst, a, b)], b - a)
+            pe([(P(d + o - a, e - o), S("e1"), S("w", o, e)), (P(d + o - a, e - o), S("en1", 0, 128), S(src, o, e))], prio=0)
+        return lambda: ac(S(dst, a, b), P(d, b - a), AF.Relu)
 
-    def sums(k, h, buf, sel, alone=False, n=8):
-        return [(ps[:, k + r:k + 16 * n:16], S(buf, h * 2048 + r, h * 2048 + 2048, 16), S(sel), alone, alone or r == 15, n)
-                for r in range(16)]
+    def sums(k, h, buf, sel):
+        n = width(sel)
+        return [(P(k + r, 16 * n - r, 16), S(buf, h * 2048 + r, h * 2048 + 2048, 16), sel) for r in range(16)]
 
-    def key(k, h, buf, is_min, d, more=(), prio=1, split=False):
-        out = ps[:, k:k + 128]
-        n = 1 if d == 0 else 2
-        sign = "gn" if is_min else "gp"
-        mms = [(out, T.one[0:n, :], T["coo" if d is None else "con"][0:n, :], True, False, 128)]
-        rd = [R("one"), R("con"), R("coo"), R("e1")] + list(more)
-        a = h * 128
-        if not is_min:
-            mms.append((out, S("en1", 0, 128), S("whi", a, a + 128), False, False, 128))
-            mms.append((out, S("en1", 0, 128), S("wlo", a, a + 128), False, False, 128))
-            rd += [R("en1", 0, 128), R("whi"), R("wlo")]
-        if d is None:
-            mms.append((out, S("ahi", a, a + 128), S("e16"), False, False, 128))
-            mms.append((out, S("alo", a, a + 128), S("e1"), False, False, 128))
-            rd += [R("ahi"), R("alo"), R("e16")]
-        else:
-            a += d * 256
-            mms.append((out, S("chi", a, a + 128), S("e1"), False, False, 128))
-            mms.append((out, S("clo", a, a + 128), S("e1"), False, False, 128))
-            rd += [R("chi"), R("clo")]
-        if split:
-            pe(mms, rd, [P(k, 128)], prio)
-            mms, rd = [], []
-        pe(mms + sums(k, h, buf, sign), rd + [R(buf, h * 2048, h * 2048 + 2048), R(sign)], [P(k, 128)], prio)
+    def wrap(k, src, a, b, sel):
+        return [(P(k, (b - a) // 16), S(sel, 15 - r, 143 - r), S(src, a + r, b, 16)) for r in range(16)]
 
-    def wrap(k, src, a, b, sel, first, last):
-        n = (b - a) // 16
-        return [(ps[:, k:k + n], S(sel, 15 - r, 143 - r), S(src, a + r, b, 16), first and r == 0, last and r == 15, n)
-                for r in range(16)]
+    def half(name, h, o=0):
+        return S(name, o + h * 128, o + h * 128 + 128)
 
-    hcore = helpers(T, topo)[core]
+    tab = "x00"
     for t in range(2):
-        z, zn, xo, x2 = "z%d" % t, "z%d" % (t + 1), "xo%d" % t, "x2%d" % t
-        ZW = R(z, 0, V)
+        z, zn = "z%d" % t, "z%d" % (t + 1)
+        x = [mins(d, t) for d in range(5)]
 
-        def vmin(d, dst, a, b):
-            tt(S(dst, a, b), ind(z, V, "cu", d * V + a, d * V + b), S("w", a, b), A.min,
-               [ZW, R("cu"), R("w", a, b)], [R(dst, a, b)], (b - a) * GA)
+        def turned_key(d, h, place=1, split=False):
+            k = KEY[d][h]
+            out = P(k, 128)
+            relus = d == 2 and (2, h * 2048, h * 2048 + 1024) not in FOLDS[t]
+            if relus:
+                mms = [(out, S("e1"), half("whi", h)), (out, S("e1"), half("wlo", h))]
+            else:
+                mms = [(out, S("con", 128 - 128 * place, 256 - 128 * place, p=two), S("one", 0, 128, p=two))]
+            mms.append((out, half("c16", h, d * 256), S("eh")))
+            if split:
+                pe(mms, last=False)
+                mms = []
+            pe(mms + sums(k, h, x[d], S("gp" if relus else "gn")), first=not split)
 
-        def sgather(d, dst, a, b):
-            ac(S(dst, a, b), ind(z, V, "cu", d * V + a, d * V + b), AF.Copy, [ZW, R("cu")], [R(dst, a, b)], (b - a) * GA)
+        def vmin(d, a, b):
+            tt(S(x[d], a, b), ind(z, V, "cu", d * V + a, d * V + b), S("w", a, b), A.min)
 
-        def merge(src, k, a, b):
-            tt(S("bi", a, b), S(src, a, b), ps[:, k:k + b - a], A.min, [R(src, a, b), P(k, b - a)], [R("bi", a, b)], b - a)
+        def sgather(d, a, b):
+            ac(S("zg%d" % d, a, b), ind(z, V, "cu", d * V + a, d * V + b))
 
-        def clear(a=0, b=256):
-            ts(S("bj", a, b), S("bi", a, b), -4097, None, A.bitwise_and, None, [R("bi", a, b)], [R("bj", a, b)], b - a)
+        def chain(h):
+            def merge(dst, src, d):
+                return lambda: tt(half(dst, h), half(src, h), P(KEY[d][h], 128), A.min)
 
-        def parts(h):
-            a, b = h * 128, h * 128 + 128
-            merge("bj", K3[h], a, b)
-            clear(a, b)
-            merge("bj", KO[h], a, b)
-            ts(S("hli", 2 * a, 2 * a + 128), S("bi", a, b), 4, 255, A.arith_shift_right, A.bitwise_and,
-               [R("bi", a, b)], [R("hli", 2 * a, 2 * a + 128)], 128)
-            ts(S("hli", 2 * a + 128, 2 * b), S("bi", a, b), 15, None, A.bitwise_and, None,
-               [R("bi", a, b)], [R("hli", 2 * a + 128, 2 * b)], 128)
-            cp(S("hl", 2 * a, 2 * b), S("hli", 2 * a, 2 * b), [R("hli", 2 * a, 2 * b)], [R("hl", 2 * a, 2 * b)], 256)
+            def clear():
+                ts(half("bj", h), half("bi", h), -4097, None, A.bitwise_and)
 
-        mine = "o0" not in FOLDS[t]
-        far = "g0" in FOLDS[t]
-        pre = PRE if t == 0 else 0
-        if pre:
-            cp(S("zg3", V - pre, V), ind(z, V, "cu", 4 * V - pre, 4 * V), [ZW, R("cu")], [R("zg3", V - pre, V)], pre * GA)
-        for a, b in (wb if t == 0 else blocks(0, V)):
-            vmin(0, "x0", a, b)
-        sgather(2, "zg2", 0, 1024)
-        sgather(2, "zg2", 1024, 2048)
-        eng = topo.engines(core, hcore)
-        for f in FOLDS[t]:
-            dst, a, b = folded(f, t)
-            src = z if f[0] == "o" else "zg2"
+            def own():
+                merge("pf", "bj", 4)()
+                pe([(P(KP, 128), half("pf", h), S("ef"))])
 
-            def fold(g, name=f + str(t), a=a, b=b, src=src, dst=dst, eng=eng):
-                rid, pid, _ = topo.addr(hcore)
-                g.remote_dma_fused([RemoteDMATransfer(dst_ids=[DstId(rid=rid, pnc=pid)], dma_engine_mask=sum(1 << e for e in eng),
-                                                      remote_sem=T.sem["out" + name], srcs=[S(src, a, b), S("w", a, b)],
-                                                      dsts=[S(dst, a, b)], alu_op=3)], local_sem=T.sem["sent"])
-                return None
-            add("pool", fold, [R(src, a, b), R("w", a, b), R("w", 2048, 3072)], [R("net" + f + str(t))], 0.5, sem="sent",
-                lat=1.3, inc=len(eng))
-            add("net", None, [R("net" + f + str(t))], [R(dst, a, b)], 3.0, sem="back" + f + str(t), inc=len(topo.engines(hcore, core)))
-        if not far:
-            short("zg2", x2, 0, 1024)
-        if mine:
-            short(z, xo, 0, 1024)
-        sgather(2, "zg2", 2048, 3072)
+            def turn():
+                cp(S("ht"), S("hti"))
+                for i in range(2):
+                    pe([(P(KT + i * 128, 128), half("ht", i), S("e1"))])
+                for i in range(2):
+                    ac(half("hl", 0, i * 256), P(KT + i * 128, 128))
+            out = ("hti", "hli")[h]
+            parts = [merge("bi", "bj", 3), lambda: ts(half(out, h), half("bi", h), 4, 255, A.arith_shift_right, A.bitwise_and),
+                     lambda: ts(half(out, 1, 256 * h), half("bi", h), 15, None, A.bitwise_and)]
+            if h == 0:
+                return [merge("bi", "b0", 4), clear, merge("bi", "bj", 1), clear, merge("bi", "bj", 2), clear] + parts + [turn]
+            return ([merge("bi", "b0", 1), clear, merge("bi", "bj", 2), clear, own,
+                     lambda: ts(half("bi", h), P(KP, 128), 4096.0, None, A.add), clear] + parts
+                    + [lambda i=i: cp(half("hl", h, i), half("hli", h, i)) for i in (0, 256)])
+
+        relu = [None]
+
+        def scalar_block(d=None, a=0, b=0):
+            last = relu[0]
+            relu[0] = None
+            if d:
+                sgather(d, a, b)
+                if (d, a, b) not in FOLDS[t]:
+                    relu[0] = short("zg%d" % d, x[d], a, b)
+            if last:
+                last()
+
+        def key3():
+            out = P(KEY[3][1], 128)
+            pe([(out, S("eh"), half("c16", 1, 768))] + [(out, half(y, 1), S("e1")) for y in ("whi", "wlo")], last=False)
+
+        def sum3(a, b, last=False):
+            pe(wrap(KEY[3][1] - 128 + a // 16, x[3], a, b, "skp"), first=False, last=last)
+        A0, B0 = chain(0), chain(1)
+        for q in range(1 - t, len(FOLDS[t])):
+            fold(t, q, 0)
+        for a, b in blocks(0, 2048):
+            scalar_block(2, a, b)
+        for a, b in ((0, 768), (768, 2048)) if t == 0 else ((0, 2048),):
+            vmin(0, a, b)
+            vmin(1, a, b)
         if t == 0:
-            for h in range(2):
-                pe(sums(KW + h * 128, h, "w", "gp", True), [R("w", h * 2048, h * 2048 + 2048), R("gp")], [P(KW + h * 128, 128)], 0)
-            ac(S("whi"), ps[:, KW:KW + 256], AF.Copy, [P(KW, 256)], [R("whi")], 256)
-            tt(S("wlo"), ps[:, KW:KW + 256], S("whi"), A.subtract, [P(KW, 256), R("whi")], [R("wlo")], 256)
-        if not far:
-            short("zg2", x2, 1024, 2048)
-        if mine:
-            short(z, xo, 1024, 2048)
-        for a, b in blocks(0, V):
-            vmin(1, "x1", a, b)
-        for h in range(2):
-            key(K0 + h * 128, h, "x0", True, 0)
-        sgather(2, "zg2", 3072, V)
-        if far:
-            short("zg2", x2, 2048, 3072)
-        ac(S("b0"), ps[:, K0:K0 + 256], AF.Copy, [P(K0, 256)], [R("b0")], 256)
-        dma("sp", "da%d" % t, T.x0[2:128:16, :], S("ahi"), [R("ahi"), R("b0"), R("x0")], [R("t1a")], 64e3)
-        dma("sp", "db%d" % t, T.x0[3:128:16, :], S("alo"), [R("alo"), R("b0"), R("x0")], [R("t1b")], 64e3)
-        if not far:
-            short("zg2", x2, 2048, 3072)
-        sgather(3, "zg3", 2048, 3072)
-        short("zg2", x2, 3072, V)
-        for h in range(2):
-            key(K2 + h * 128, h, x2, far and h == 0, 2, more=[R("x1", 1024, 2048)] if far else [])
-            key(K1 + h * 128, h, "x1", True, 1, prio=-1)
-        sgather(3, "zg3", 3072, V - pre)
-        short("zg3", "x3", 2048, 3072)
-        short("zg3", "x3", 3072, V)
-        vmin(3, "x3", 0, CUTS[0])
-        merge("b0", K1, 0, 256)
-        vmin(3, "x3", CUTS[0], CUTS[1])
-        clear()
-        merge("bj", K2, 0, 256)
-        vmin(3, "x3", CUTS[1], 2048)
-        clear()
-        key(KO[1], 1, xo, True, None, more=[R("x1", 2048, 3072)])
-        key(KO[0], 0, xo, not mine, None, more=[] if mine else [R("x1")])
-        key(K3[1], 1, "x3", False, 3, split=True)
-        key(K3[0], 0, "x3", True, 3, more=[P(KO[0], 128)], split=True)
-        n0 = len(ops)
-        parts(1)
-        n1 = len(ops)
-        parts(0)
-        one, two = ops[n0:n1], ops[n1:]
-        ops[n0:] = [o for pair in zip(one, two) for o in pair]
-
-        def turn(k, terms, own=False):
-            mms = []
-            for h in range(2):
-                out = ps[:, k + h * 128:k + h * 128 + 128]
-                lst = [(S("hl", h * 256 + p * 128, h * 256 + p * 128 + 128), S(e, 0, 128)) for p, e in terms]
-                if own:
-                    lst += [(S("e16"), S("ahi", h * 128, h * 128 + 128)), (S("e1"), S("alo", h * 128, h * 128 + 128))]
-                for i, (l, r_) in enumerate(lst):
-                    mms.append((out, l, r_, i == 0, i == len(lst) - 1, 128))
-            pe(mms, [R("hl"), R("e1"), R("e16"), R("ahi"), R("alo")] + [R(e, 0, 128) for p, e in terms], [P(k, 256)])
-        turn(0, [(0, "e1")])
-        turn(1024, [(1, "e1")])
-        turn(512, [(0, "e1"), (1, "e256")])
-        turn(1536, [(0, "en16"), (1, "en1")], own=True)
-        turn(1792, [(0, "e16"), (1, "e1")])
-        ac(S("fh"), ps[:, 0:256], AF.Copy, [P(0, 256)], [R("fh")], 256)
-        cp(S("fl"), ps[:, 1024:1280], [P(1024, 256)], [R("fl")], 256)
-        dma("act", "dh%d" % t, T.x0[0:128:16, :], S("fh"), [R("fh"), R("x0")], [R("t1h")], 64e3)
-        dma("sp", "dl%d" % t, T.x0[1:128:16, :], S("fl"), [R("fl"), R("x0")], [R("t1l")], 64e3)
-        cp(S("lf"), ps[:, 512:768], [P(512, 256)], [R("lf")], 256)
-        ac(S("di", 0, 512, 2), ps[:, 1536:1792], AF.Copy, [P(1536, 256)], [R("di")], 256)
-        ac(S("di", 1, 512, 2), ps[:, 1792:2048], AF.Copy, [P(1792, 256)], [R("di")], 256)
+            pe([(P(KW, 256), S("con", 0, 128, p=two), S("one", p=two))] + sums(KW, 0, "w", S("gn")), last=False)
+        turned_key(0, 0)
         if t == 0:
-            late_constants()
+            pe(sums(KW + 128, 1, "w", S("gn")), first=False)
+        scalar_block(2, 2048, 3072)
+        turned_key(1, 0)
+        if t == 0:
+            vmin(0, 2048, 3072)
+            ac(S("whi"), P(KW, 256))
+            tt(S("wlo"), P(KW, 256), S("whi"), A.subtract)
+        turned_key(2, 0)
+        scalar_block(2, 3072, V)
+        vmin(0, 3072 - 1024 * t, V)
+        turned_key(0, 1, 0)
+        if t == 0:
+            move("sp", "da", S(tab, p=(2, 128, 16)), S("ahi"))
+            move("sp", "db", S(tab, p=(3, 128, 16)), S("alo"))
+        turned_key(4, 0, 0)
+        scalar_block(3, 2048, 3072)
+        vmin(1, 2048, V)
+        turned_key(1, 1)
+        turned_key(2, 1)
+        last, relu[0] = relu[0], None
+        scalar_block(3, 3072, V)
+        ac(S("b0"), P(KEY[0][0], 256))
+        last()
+        scalar_block()
+        turned_key(4, 1, -1)
+        vmin(3, 0, 2048)
+        turned_key(3, 0)
+        A0[0]()
+        B0[0]()
+        key3()
+        sum3(2048, 3072)
+        for step in [s for pair in zip(A0[1:5], B0[1:5]) for s in pair]:
+            step()
+        sum3(3072, V, True)
+        for step in [A0[5], A0[6], B0[5], A0[7], B0[6], A0[8], A0[9]] + B0[7:]:
+            step()
+        move("sp", "dh%d" % t, S(tab, p=(0, 128, 16)), S("hl", 0, 256))
+        move("act", "dl%d" % t, S(tab, p=(1, 128, 16)), S("hl", 256, 512))
+        pe([(P(KF, 256), S("e1"), S("hl", 0, 256)), (P(KF, 256), S("e256"), S("hl", 256, 512))])
+        cp(S("lf"), P(KF, 256))
+        pe([(P(0, 512, 2), S("e16"), S("ahi")), (P(0, 512, 2), S("e1"), S("alo")),
+            (P(0, 512, 2), S("en16", 0, 128), S("hl", 0, 256)), (P(0, 512, 2), S("en1", 0, 128), S("hl", 256, 512))])
+        pe([(P(513, 511, 2), S("e16"), S("hl", 0, 256)), (P(513, 511, 2), S("e1"), S("hl", 256, 512))])
+        ac(S("di", 0, 512, 2), P(0, 512, 2))
+        ac(S("di", 1, 512, 2), P(513, 511, 2))
 
-        XY = (3072, 3584)
+        XY, KG, KU = (1024, 1536), (2048, 2560), (3072, 3584)
         for h in range(2):
-            pe([(ps[:, XY[h]:XY[h] + 256], S("ahi", h * 128, h * 128 + 128), S("en16"), True, False, 256),
-                (ps[:, XY[h]:XY[h] + 256], S("alo", h * 128, h * 128 + 128), S("en1"), False, False, 256)],
-               [R("ahi"), R("alo"), R("en1"), R("en16"), R("hl")], [P(XY[h], 256)])
+            pe([(P(XY[h], 256), half("ahi", h), S("en16")), (P(XY[h], 256), half("alo", h), S("en1"))], last=False, prio=2)
 
-        def both(win, wres, lst, dst, q, n=512):
-            a, m, b = q * 1024, q * 1024 + n, q * 1024 + 1024
-            cp(S(dst, a, m), ind(win, V, lst, a, m), wres + [R(lst, a // 16, m // 16)], [R(dst, a, m)], n * GA)
-            ac(S(dst, m, b), ind(win, V, lst, m, b), AF.Copy, wres + [R(lst, m // 16, b // 16)], [R(dst, m, b)], (1024 - n) * GA)
-        for q in range(4):
-            both("x0", [R("x0"), R("t1h"), R("t1l"), R("t1a"), R("t1b")], "lf", "t2", q)
-            k = 2048 + q * 64 if q < 3 else 2560
-            pe(wrap(k, "t2", q * 1024, q * 1024 + 1024, "s1w", True, True), [R("t2", q * 1024, q * 1024 + 1024), R("s1w")], [P(k, 64)])
-        cp(S("lg", 0, 192), ps[:, 2048:2240], [P(2048, 192)], [R("lg", 0, 192)], 192)
-        both("t2", [R("t2")], "lg", "t3", 0, G2[0])
-        cp(S("lg", 192, 256), ps[:, 2560:2624], [P(2560, 64)], [R("lg", 192, 256)], 64)
-        both("t2", [R("t2")], "lg", "t3", 1, G2[1])
-        for h in range(2):
-            a, k = h * 128, K3[h]
-            both("t2", [R("t2")], "lg", "t3", 2 + h, G2[2 + h])
-            pe(sums(XY[h], h, "t3", "sxy", n=16), [R("t3", h * 2048, h * 2048 + 2048), R("sxy")], [P(XY[h], 256)])
-            ts(S("nn", 2 * a, 2 * a + 256), ps[:, XY[h]:XY[h] + 256], 0.0, None, A.not_equal, None,
-               [P(XY[h], 256)], [R("nn", 2 * a, 2 * a + 256)], 256)
-            if h:
-                cp(S("fi", 1, 256, 2), ps[:, K3[0]:K3[0] + 128], [P(K3[0], 128)], [R("fi", 0, 256)], 128)
-            tt(S("ft", a, a + 128), S("nn", 2 * a, 2 * a + 128), S("nn", 2 * a + 128, 2 * a + 256), A.mult,
-               [R("nn", 2 * a, 2 * a + 256)], [R("ft", a, a + 128)], 256)
-            pe([(ps[:, k:k + 128], S("ft", a, a + 128), S("e1"), True, True, 128)], [R("ft", a, a + 128), R("e1")], [P(k, 128)])
-        ac(S("fi", 257, 512, 2), ps[:, K3[1]:K3[1] + 128], AF.Copy, [P(K3[1], 128)], [R("fi", 256, 512)], 128)
-        for k, m, nm in ((0, "bd", "nbd"), (1024, "tri", "ntri")):
-            pe([(ps[:, k + 256:k + 272], S(m), S("one", 0, 16), True, False, 16),
-                (ps[:, k + 256:k + 272], S(nm), S("fi", 1, 32, 2), False, True, 16),
-                (ps[:, k:k + 128], S(m), S("fi", 1, 256, 2), True, True, 128)],
-               [R("fi", 0, 256), R(m), R(nm), R("one")], [P(k, 272)])
-        for k, m in ((128, "bd"), (1152, "tri")):
-            pe([(ps[:, k:k + 128], S(m), S("fi", 257, 512, 2), True, True, 128)], [R("fi", 256, 512), R(m)], [P(k, 128)])
-        scan(S("pp"), S("fi"), S("di"), A.mult, A.add, [R("fi"), R("di")], [R("pp")], 512)
-        scan(S("eb", 1, 273), ps[:, 0:272], S("c256"), A.add, A.min, [P(0, 272), R("c256")], [R("eb", 1, 273)], 272)
-        pe([(ps[:, 512:528], S("s3w", 15 - r, 143 - r), S("eb", 1 + r, 1 + r + 256, 17), r == 0, r == 15, 16) for r in range(16)],
-           [R("eb"), R("s3w")], [P(512, 16)])
-        ac(S("tb"), ps[:, 512:528], AF.Copy, [P(512, 16)], [R("tb")], 16, scale=0.0625)
-        tt(S("m1"), ind("eb", 273, "l1", 0, 256), S("k1"), A.is_le, [R("eb"), R("l1"), R("k1")], [R("m1")], 256 * GA)
-        scan(S("s1"), S("kp"), S("m1"), A.mult, A.add, [R("kp"), R("m1")], [R("s1")], 128)
-        cp(S("l2"), S("s1", 15, 256, 16), [R("s1")], [R("l2")], 16)
-        tt(S("m2"), ind("tb", 16, "l2", 0, 256), S("ahi"), A.is_le, [R("tb"), R("l2"), R("ahi")], [R("m2")], 256 * GA)
-        pe([(ps[:, 3072:3088], S("e17"), S("s1", 15, 256, 16), True, False, 16)] + wrap(3072, "m2", 0, 256, "s3w", False, True),
-           [R("s1"), R("m2"), R("e17"), R("s3w")], [P(3072, 16)])
-        pe([(ps[:, 3584:3600], S("e272"), S("s1", 15, 256, 16), True, False, 16)] + wrap(3584, "m2", 0, 256, "s4w", False, False),
-           [R("s1"), R("m2"), R("e272"), R("s4w")], [P(3584, 16)])
-        cp(S("lp"), S("pp", 1, 512, 2), [R("pp")], [R("lp")], 256)
-        tt(S("pin"), S("eb", 0, 272), ps[:, 1024:1296], A.add, [R("eb"), P(1024, 272)], [R("pin")], 272)
-        cp(S("l3"), ps[:, 3072:3088], [P(3072, 16)], [R("l3")], 16)
-        tt(S("m3"), ind("pin", 272, "l3", 0, 256), S("ahi"), A.is_le, [R("pin"), R("l3"), R("ahi")], [R("m3")], 256 * GA)
-        pe(wrap(3584, "m3", 0, 256, "s3w", False, True), [R("m3"), R("s3w")], [P(3584, 16)])
-        cp(S(z, V, V + 256), ind(z, V, "lp", 0, 256), [ZW, R("lp")], [R(z, V, V + 256)], 256 * GA)
-        cp(S("lv"), ps[:, 3584:3600], [P(3584, 16)], [R("lv")], 16)
-        away, land = "away%d" % t, "land%d" % t
-        cp(S(away), ind(z, V + 256, "lv", 0, 256), [R(z), R("lv")], [R(away)], 256 * GA)
+        def both(win, lst, dst, a, n, b):
+            cp(S(dst, a, a + n), ind(win, V, lst, a, a + n))
+            ac(S(dst, a + n, b), ind(win, V, lst, a + n, b))
+        for q, (a, b) in enumerate(blocks(0, V)):
+            if q == 3:
+                cp(S("lg", 0, 128), P(KG[0], 128))
+            both(tab, "lf", "t2", a, G1[q], b)
+            pe(wrap(KG[q // 2] + q % 2 * 64, "t2", a, b, "s1w"))
+        both("t2", "lg", "t3", 0, G2[0], 2048)
+        cp(S("lg", 128, 256), P(KG[1], 128))
+
+        def differs(h):
+            ts(S("nn", h * 256, h * 256 + 256), P(XY[h], 256), 0.0, None, A.not_equal)
+            pe([(P(KU[h], 128), half("nn", 2 * h + i), S("e1")) for i in range(2)])
+
+        def unmet(h):
+            ts(S("fi", h * 256 + 1, h * 256 + 256, 2), P(KU[h], 128), 1.5, None, A.is_ge)
+
+        def trades(h):
+            scan(S("pp", h * 256, h * 256 + 256), S("fi", h * 256, h * 256 + 256), S("di", h * 256, h * 256 + 256), A.mult, A.add)
+
+        def trade_list(h):
+            cp(half("lp", h), S("pp", h * 256 + 1, h * 256 + 256, 2))
+        pe(sums(XY[0], 0, "t3", S("sxy")), first=False)
+        m = 2048 + G2[1] + G2[2]
+        ac(S("t3", m, V), ind("t2", V, "lg", m, V))
+        cp(S("t3", 2048, 2048 + G2[1]), ind("t2", V, "lg", 2048, 2048 + G2[1]))
+        differs(0)
+        cp(S("t3", 2048 + G2[1], m), ind("t2", V, "lg", 2048 + G2[1], m))
+        pe(sums(XY[1], 1, "t3", S("sxy")), first=False)
+        unmet(0)
+        trades(0)
+        KN = (0, 512)
+        pe([(P(KN[0], 128), S("bd"), S("fi", 1, 256, 2))])
+        pe([(P(KN[1] + 128, 16), S("bd"), S("one", 0, 16)), (P(KN[1] + 128, 16), S("nbd"), S("fi", 1, 32, 2))])
+        differs(1)
+        trade_list(0)
+        ac(S(zn, 0, 2048), ind(z, V, "lp", 0, 2048))
+        scan(S("eb", 1, 129), P(KN[0], 128), S("c256", 0, 128), A.add, A.min)
+        unmet(1)
+        pe([(P(KN[1], 128), S("bd"), S("fi", 257, 512, 2))])
+        pe([(P(XY[0], 256), S("tri"), S("fi", 1, 512, 2))])
+        pe([(P(XY[0] + 256, 16), S("tri"), S("one", 0, 16)), (P(XY[0] + 256, 16), S("ntri"), S("fi", 1, 32, 2))])
+        scan(S("eb", 129, 273), P(KN[1], 144), S("c256", 0, 144), A.add, A.min, S("eb", 128, 129))
+        pe([(P(KG[0], 16), S("s3w", 15 - r, 143 - r), S("eb", 1 + r, 1 + r + 256, 17)) for r in range(16)])
+        tt(S("m1"), ind("eb", 273, "l1", 0, 256), S("k1"), A.is_le)
+        ts(S("tb"), P(KG[0], 16), 0.0625, None, A.mult)
+        scan(S("s1"), S("kp"), S("m1"), A.mult, A.add)
+        cp(S("l2"), S("s1", 15, 256, 16))
+        tt(S("m2"), ind("tb", 16, "l2", 0, 256), S("ahi"), A.is_le)
+        KC, KV = KG[1], KU[0]
+        pe([(P(KC, 16), S("e17"), S("s1", 15, 256, 16))], last=False)
+        pe([(P(KV, 16), S("e272"), S("s1", 15, 256, 16))], last=False)
+        pe(wrap(KC, "m2", 0, 256, "s3w"), first=False, prio=0)
+        pe(wrap(KV, "m2", 0, 256, "s4w"), first=False, last=False)
+        trades(1)
+        tt(S("pin"), S("eb", 0, 272), P(XY[0], 272), A.add)
+        cp(S("l3"), P(KC, 16))
+        tt(S("m3"), ind("pin", 272, "l3", 0, 256), S("ahi"), A.is_le)
+        pe(wrap(KV, "m3", 0, 256, "s3w"), first=False)
+        trade_list(1)
+        ac(S(zn, 2048, ZS), ind(z, V, "lp", 2048, ZS))
+        cp(S(z, V, V + 256), ind(z, V, "lp", 0, 256))
+        cp(S("lv"), P(KV, 16))
+        away, land = S("away%d" % t), S("land%d" % t)
+        cp(away, ind(z, V + 256, "lv", 0, 256))
         dst = T.cores[(rank + 1 + t) % n_ranks]
         eng = topo.engines(core, dst)
         got = len(topo.engines(T.cores[(rank - 1 - t) % n_ranks], core))
+        net = ("net%d" % t, 0, 1, 1, 0, 1, 1)
 
         def send(g, t=t, dst=dst, eng=eng, away=away, land=land):
             rid, pid, _ = topo.addr(dst)
-            g.remote_dma(S(land), S(away), T.sem["arr%d" % t], T.sem["sent"], pid, rid, sum(1 << e for e in eng))
+            g.remote_dma(ap(land), ap(away), T.sem["arr%d" % t], T.sem["sent"], pid, rid, sum(1 << e for e in eng))
             return None
-        add("pool", send, [R(away)], [R("net%d" % t)], 0.3, sem="sent", lat=0.3, inc=len(eng))
-        add("net", None, [R("net%d" % t)], [R(land)], 0.0, sem="arr%d" % t, inc=got)
-        for a, b in blocks(0, ZS):
-            ac(S(zn, a, b), ind(z, V, "lp", a, b), AF.Copy, [ZW, R("lp")], [R(zn, a, b)], (b - a) * GA)
-        cp(S("oi"), ps[:, 3584:3600], [P(3584, 16)], [R("oi")], 16)
-        cp(S(zn, ZS, V - 512), ind(z, V, "lp", ZS, V - 512), [ZW, R("lp")], [R(zn, ZS, V - 512)], (V - 512 - ZS) * GA)
-        ts(S("oj"), S("oi"), 4095, None, A.bitwise_and, None, [R("oi")], [R("oj")], 16)
-        cp(S(zn, V - 512, V), ind(z, V, "lp", V - 512, V), [ZW, R("lp")], [R(zn, V - 512, V)], 512 * GA)
-        cp(S("lo"), S("oj"), [R("oj")], [R("lo")], 16)
-        cp(ind(zn, V, "lo", 0, 256), S(land), [R(land), R("lo")], [R(zn, 0, V)], 256 * SC)
-    dma("sp", "dy0", T.y[:, 0:2048], S("z2", 0, 2048), [R("z2")], [R("y", 0, 1)], 512e3)
-    dma("act", "dy1", T.y[:, 2048:V], S("z2", 2048, V), [R("z2")], [R("y", 1, 2)], 512e3)
+        add("pool", send, [away], [net], 0.1, sem="sent", lat=ROWS + 65536 / DRATE, inc=len(eng))
+        add("net", None, [net], [land], 0.0, sem="arr%d" % t, inc=got)
+        cp(S("oi"), P(KV, 16))
+        cp(S(zn, ZS, V), ind(z, V, "lp", ZS, V))
+        ts(S("oj"), S("oi"), 4095, None, A.bitwise_and)
+        cp(S("lo"), S("oj"))
+        cp(ind(zn, V, "lo", 0, 256), land)
+    dma("sp", "dy0", T.y[:], T.z2[:], [S("z2")], [("y", 0, 1, 1, 0, 1, 1)], 1024e3)
     return ops
 
 
 def _meet(x, y):
-    return x[0] == y[0] and x[1] < y[2] and y[1] < x[2]
+    if x[0] != y[0] or x[1] >= y[2] or y[1] >= x[2] or (x[3] == y[3] and (x[1] - y[1]) % x[3]):
+        return False
+    return not (x[6] == y[6] and (x[4] - y[4]) % x[6])
 
 
 def _banks(o):
@@ -438,56 +483,84 @@ def _banks(o):
 def order(ops):
     n = len(ops)
     banks = [_banks(o) for o in ops]
+    names = [(set(x[0] for x in o["wr"]), set(x[0] for x in o["rd"] + o["wr"])) for o in ops]
     deps = [[] for _ in ops]
     prev = [None] * n
     last = {}
     for j in range(n):
         b = ops[j]
-        if b["q"] not in ("pe", "net"):
+        if b["q"] not in LOOSE:
             prev[j] = last.get(b["q"])
             last[b["q"]] = j
         for i in range(j):
             a = ops[i]
-            if (any(_meet(x, y) for x in a["wr"] for y in b["rd"] + b["wr"]) or any(_meet(x, y) for x in a["rd"] for y in b["wr"])
-                    or (a["q"] != b["q"] and banks[i] & banks[j])):
+            if banks[i] & banks[j] and a["q"] == b["q"] == "pe" and (a["part"] or b["part"]):
                 deps[j].append(i)
-    done = [None] * n
-    free = {}
-    ring = 0.0
-    seq = []
-    left = list(range(n))
-    while left:
-        best = None
-        for j in left:
-            if (prev[j] is not None and done[prev[j]] is None) or any(done[i] is None for i in deps[j]):
-                continue
-            st = max([free.get(ops[j]["q"], 0.0)] + [done[i] + WAKE for i in deps[j]])
-            k = (round(st / 0.2), ops[j]["prio"], j)
-            if best is None or k < best[0]:
-                best = (k, j, st)
-        _, j, st = best
-        o = ops[j]
-        if o["q"] != "net":
-            free[o["q"]] = st + o["cost"]
-        if o["sem"] and o["q"] != "net":
-            ring = max(ring, st + DLAT) + o["lat"]
-            done[j] = ring
-        else:
-            done[j] = st + o["cost"]
-        left.remove(j)
-        seq.append(j)
-    return seq, deps
+            elif (names[i][0] & names[j][1] or names[i][1] & names[j][0]) and (
+                    any(_meet(x, y) for x in a["wr"] for y in b["rd"] + b["wr"]) or any(_meet(x, y) for x in a["rd"] for y in b["wr"])):
+                deps[j].append(i)
+    seq, best = list(range(n)), None
+    if not PASSES:
+        return seq, [deps[j] + [i for i in range(j) if banks[i] & banks[j] and ops[i]["q"] != ops[j]["q"]] for j in seq]
+    for again in range(PASSES):
+        rest = [0.0] * n
+        behind = {}
+        for j in reversed(seq):
+            q = ops[j]["q"]
+            if q != "net" and (again or q != "pe"):
+                rest[j] = max(rest[j], behind.get(q, 0.0))
+            rest[j] += ops[j]["cost"]
+            behind[q] = rest[j]
+            rest[j] += DLAT + ops[j]["lat"] if ops[j]["sem"] and q != "net" else 0.0
+            for i in deps[j]:
+                rest[i] = max(rest[i], rest[j] + WAKE)
+        user = {}
+
+        def others(j):
+            return [i for (b, q), i in user.items() if b in banks[j] and q != ops[j]["q"]]
+        done = [None] * n
+        free = {}
+        ring = 0.0
+        seq, full = [], [None] * n
+        left = list(range(n))
+        while left:
+            ready = []
+            for j in left:
+                if (prev[j] is not None and done[prev[j]] is None) or any(done[i] is None for i in deps[j]):
+                    continue
+                st = max([free.get(ops[j]["q"], 0.0)]
+                         + [done[i] + (0 if ops[i]["q"] == ops[j]["q"] == "pe" else WAKE) for i in deps[j] + others(j)])
+                ready.append((st, j))
+            st, j = min(ready)
+            q = ops[j]["q"]
+            st, j = max([x for x in ready if x[0] <= st + AHEAD and ops[x[1]]["q"] == q], key=lambda x: rest[x[1]] - x[0])
+            o = ops[j]
+            full[j] = deps[j] + others(j)
+            for b in banks[j]:
+                user[b, q] = j
+            if q != "net":
+                free[q] = st + o["cost"]
+            if o["sem"] and q != "net":
+                ring = max(ring, st + (RLAT if q == "pool" else DLAT)) + o["lat"]
+                done[j] = ring
+            else:
+                done[j] = st + o["cost"]
+            left.remove(j)
+            seq.append(j)
+        if best is None or max(done) < best[0]:
+            best = (max(done), seq, full)
+    return best[1:]
 
 
 def hand_back(g, core, home, T, topo):
     rid, pid, _ = topo.addr(home)
     eng = topo.engines(core, home)
     for t in range(2):
-        for f in FOLDS[t]:
-            buf, a, b = folded(f, t)
-            g.wait_ge(T.sem["out" + f + str(t)], len(topo.engines(home, core)))
-            g.remote_dma(T[buf][:, a:b], T[buf][:, a:b], T.sem["back" + f + str(t)], T.sem["sent"], pid, rid, sum(1 << e for e in eng))
-    g.wait_ge(T.sem["sent"], sum(len(f) for f in FOLDS) * len(eng))
+        for q, (d, a, b) in enumerate(FOLDS[t]):
+            x = T[mins(d, t)][:, a:b]
+            g.wait_ge(T.sem["out%d%d" % (t, q)], len(topo.engines(home, core)))
+            g.remote_dma(x, x, T.sem["back%d%d" % (t, q)], T.sem["sent"], pid, rid, sum(1 << e for e in eng))
+    g.wait_ge(T.sem["sent"], sum(len(x) for x in FOLDS) * len(eng))
 
 
 def rank_program(g, core, T, topo):

from concourse.bass import DstId, RemoteDMATransfer
from concourse.mybir import AluOpType as A, ActivationFunctionType as AF

V = 4096
LOADS = (("z0", 0, 768, 0), ("w", 0, 768, 0), ("ci", 0, 1024, 0), ("z0", 768, V, 0), ("w", 768, 2048, 0), ("w", 2048, V, 0))
VO = 512
FOLDS = (((4, VO, 768), (4, 768, 2048), (4, 2048, 3072), (4, 3072, V)),
         ((4, 0, 1024), (4, 1024, 2048), (4, 2048, 3072), (4, 3072, V)))
G1 = (512, 512, 512, 480)
G2 = (992, 512, 416)
ZS = 3328
BASE = 2040 * 8192

BF, F16, F32, I32, U16 = "bfloat16", "float16", "float32", "int32", "uint16"
SCRATCH = {"ps": ("psum", [128, 4096], F32)}
for _dt, _names in (
        (BF, "z0:4352 z1:4352 z2:4096 w:4096 x00:4096 x01:4096 x10:4096 x20:4096 x21:4096 x30:4096 x31:4096 x40:4096 x41:4096 "
             "zg2:4096 zg3:4096 t2:4096 t3:4096 whi:256 wlo:256 hl:512 fi:512 nn:512 eb:288 pin:272 "
             "c256:272 tb:16 m1:256 s1:256 m2:256 m3:256 away0:256 away1:256 land0:256 land1:256 ahi:256 alo:256 k1:256 "
             "k1a:256 kp:256 xg:128 con:384 ht:256 one:256 e1:128 en1:256 e16:128 en16:256 e256:128 e17:128 "
             "e272:128 bd:128 nbd:128 tri:128 ntri:128 gp:8 gn:8 sxy:16 s1w:144 s3w:144 s4w:144 skp:144 skn:144"),
        (F16, "c16:1280 eh:128"),
        (F32, "b0:256 pf:256 di:512 pp:512 col:16 ef:128"),
        (I32, "ci:1024 bi:256 bj:256 hli:512 hti:256 oi:16 oj:16 pi:2"),
        (U16, "cu:1024 lf:256 lg:256 lp:256 l1:16 l2:16 l3:16 lv:16 lo:16")):
    for _x in _names.split():
        SCRATCH[_x.split(":")[0]] = ("sbuf", [128, int(_x.split(":")[1])], _dt)
SEMAPHORES = (["pe", "dve", "act", "pool", "arr0", "arr1", "sent", "da", "db", "dh0", "dl0", "dh1", "dl1", "dy0", "dy1"]
              + ["d%s%d" % x[:2] for x in LOADS]
              + ["%s%d%d" % (p, t, q) for p in ("left", "out", "back") for t in range(2) for q in range(len(FOLDS[t]))])

CY, GA, SC, PC, VFIX, SFIX, AFIX, AR, WAKE = 0.00086, 1.45, 3.5, 0.00042, 0.06, 0.08, 0.08, 1.1, 0.07
DLAT, RLAT, DRATE, ROWS, FOLD, AHEAD = 0.8, 1.6, 400e3, 0.2, 2.5, 0.4
LOOSE, PASSES = ("pe", "net"), 0


def mins(d, t):
    return "x%d%d" % (d, 0 if d == 1 else t)


def helpers(T, topo):
    out, used = {}, set(T.cores)
    for c in T.cores:
        h = [x for x in topo.cores_of(c) if x not in used and topo.die(x) == topo.die(c)][0]
        used.add(h)
        out[c] = h
    return out


def S(name, a=0, b=None, s=1, p=(0, 128, 1)):
    return (name, a, SCRATCH[name][1][1] if b is None else b, s) + p


def P(a, n, s=1):
    return S("ps", a, a + n, s)


def ind(win, n, lst, a, b):
    return ("ind", S(win, 0, n), S(lst, a // 16, b // 16))


def width(x):
    return 16 * width(x[2]) if x[0] == "ind" else len(range(x[1], x[2], x[3]))


def narrow(x):
    return SCRATCH[x[0]][2] in (BF, F16, U16)


def blocks(a, b, n=1024):
    return [(o, min(o + n, b)) for o in range(a, b, n)]


def plan(T, topo, core):
    ops = []
    rank = T.rank_of(core)
    n_ranks = len(T.cores)

    def ap(x):
        if not isinstance(x, tuple):
            return x
        if x[0] == "ind":
            return ap(x[1]).indirect(ap(x[2]))
        return T[x[0]][x[4]:x[5]:x[6], x[1]:x[2]:x[3]]

    def add(q, fn, rd, wr, cost, sem=None, lat=0.0, inc=16, part=False):
        reads, writes = [], []
        for x in rd:
            if isinstance(x, tuple):
                reads += [x[1], x[2]] if x[0] == "ind" else [x]
        for x in wr:
            if x[0] == "ind":
                reads.append(x[2])
                x = x[1]
            writes.append(x)
        ops.append({"q": q, "fn": fn, "rd": reads, "wr": writes, "cost": cost, "sem": sem, "lat": lat, "inc": inc, "part": part})

    def took(out, in_, plain, fix=VFIX):
        if "ind" in (out[0], in_[0]):
            return fix + CY * width(out) * (SC if out[0] == "ind" else GA)
        return CY * max(64, width(out) * plain)

    def fast(*xs):
        return 0.5 if all(x[0] != "ind" and narrow(x) for x in xs) else 1

    def ts(out, in0, s1, s2, op0, op1=None):
        args = (ap(out), ap(in0), ap(s1), ap(s2), op0) + (() if op1 is None else (op1,))
        add("dve", lambda g: g.vector.tensor_scalar(*args), [in0, s1, s2], [out], took(out, in0, fast(out, in0)))

    def tt(out, in0, in1, op):
        add("dve", lambda g: g.vector.tensor_tensor(ap(out), ap(in0), ap(in1), op), [in0, in1], [out],
            took(out, in0, 1 if "ps" in (in0[0], in1[0]) else 2))

    def cp(out, in_):
        add("dve", lambda g: g.vector.tensor_copy(ap(out), ap(in_)), [in_], [out], took(out, in_, fast(out, in_)))

    def scan(out, d0, d1, op0, op1, first=0.0):
        add("dve", lambda g: g.vector.tensor_tensor_scan(ap(out), ap(d0), ap(d1), ap(first), op0, op1), [d0, d1, first], [out],
            took(out, d0, fast(out, d0, d1)))

    def fill(out, val):
        add("dve", lambda g: g.vector.memset(ap(out), val), [], [out], took(out, out, fast(out)))

    def ac(out, in_, func=AF.Copy, scale=1.0, bias=None):
        kw = {"scale": ap(scale)} if bias is None else {"scale": ap(scale), "bias": ap(bias)}
        add("act", lambda g: g.scalar.activation(ap(out), ap(in_), func, **kw), [in_, scale, bias], [out],
            took(out, in_, AR, SFIX) + (0 if in_[0] == "ind" else AFIX))

    def iota(out, pat, base, cm):
        kw = {} if SCRATCH[out[0]][2] == I32 else {"allow_small_or_imprecise_dtypes": True}
        add("pool", lambda g: g.iota(ap(out), pat, base, cm, **kw), [], [out], 0.13 + 2 * width(out) * CY)

    def keep(out, in_, pat, op, cm):
        add("pool", lambda g: g.affine_select(ap(out), ap(in_), pat, op, 0.0, 0, cm), [in_], [out], 0.17 + 2 * width(out) * CY)

    def pe(mms, first=True, last=True, prio=1, more=()):
        def fn(g):
            ins = None
            for i, m in enumerate(mms):
                ins = g.tensor.matmul(ap(m[0]), ap(m[1]), ap(m[2]), first and i == 0, last and i == len(mms) - 1)
            return ins
        cost = sum(max(64, width(m[2])) * (1 if narrow(m[1]) else 4) for m in mms) * PC
        add("pe", fn, list(set(x for m in mms for x in m[1:])) + list(more), list(set(m[0] for m in mms)), cost, part=not (first and last))

    def dma(q, sem, out, in_, rd, wr, nbytes):
        add(q, lambda g: (g.sync if q == "sp" else g.scalar).dma_start(out, in_), rd, wr, 0.05, sem=sem, lat=ROWS + nbytes / DRATE)

    def move(q, sem, out, in_):
        dma(q, sem, ap(out), ap(in_), [in_], [out], 256.0 * width(in_))

    hcore = helpers(T, topo)[core]
    line = []

    def turn_of(after):
        line.append(("line", len(line), len(line) + 1, 1, 0, 1, 1))
        return [line[-1 - after]] if after and after < len(line) else [], [line[-1]]

    def load(name, src, a, b, after):
        rd, wr = turn_of(after)
        dma("sp", "d%s%d" % (name, a), ap(S(name, a, b)), src[:, a:b], rd, wr + [S(name, a, b)], (256.0, 512.0)[name == "ci"] * (b - a))

    def fold(t, q, after):
        d, a, b = FOLDS[t][q]
        srcs, dst = (S("z%d" % t if d == 4 else "zg%d" % d, a, b), S("w", a, b)), S(mins(d, t), a, b)
        eng = topo.engines(core, hcore)
        rd, wr = turn_of(after)

        def fn(g):
            rid, pid, _ = topo.addr(hcore)
            g.remote_dma_fused([RemoteDMATransfer(dst_ids=[DstId(rid=rid, pnc=pid)], dma_engine_mask=sum(1 << e for e in eng),
                                                  remote_sem=T.sem["out%d%d" % (t, q)], srcs=[ap(x) for x in srcs], dsts=[ap(dst)],
                                                  alu_op=3)], local_sem=T.sem["left%d%d" % (t, q)])
            return None
        add("pool", fn, list(srcs) + rd, wr, 0.1, sem="left%d%d" % (t, q), lat=2 * ROWS + (b - a) * 256 * FOLD / DRATE, inc=len(eng))
        add("net", None, wr, [dst], WAKE + RLAT + ROWS + (b - a) * 256 / DRATE, sem="back%d%d" % (t, q), inc=len(topo.engines(hcore, core)))
    for name, a, b, after in LOADS:
        load(name, {"ci": T.cand, "z0": T.goods, "w": T.wish}[name], a, b, after)

    def col(j):
        return S("col", j, j + 1)
    two = (0, 2, 1)
    iota(S("pi", 0, 1), [[0, 1]], 0, 1)
    iota(S("ahi"), [[1, 256]], 0, 0)
    iota(S("xg"), [[16, 8], [0, 16]], 0, 0)
    for k in range(3):
        iota(S("con", 128 * k, 128 * k + 128, p=two), [[0, 128]], BASE, 6144 - 4096 * k - BASE)
    iota(S("k1a"), [[16, 16], [0, 16]], 0, 0)
    ts(S("pi", 1, 2), S("pi", 0, 1), 15, None, A.bitwise_and)
    fill(S("one"), 1.0)
    cp(S("col", 0, 2), S("pi"))
    fill(S("c256"), 256.0)
    tt(col(2), col(0), col(1), A.subtract)
    fill(S("fi"), 0.0)
    ts(col(5), col(2), 15.0, None, A.add)
    for k in range(2):
        ts(col(6 + 3 * k), col(1), 2.0 * k, 16.0, A.is_equal, A.mult)
        ts(col(7 + 3 * k), col(1), 2.0 * k + 1, None, A.is_equal)
    for k in range(2):
        tt(col(8 + 3 * k), col(6 + 3 * k), col(7 + 3 * k), A.add)
    fill(S("eb", 0, 1), 0.0)
    ts(S("e1"), S("ahi", 0, 128), col(0), None, A.is_equal)
    ts(S("eh"), S("ahi", 0, 128), col(0), None, A.is_equal)
    ts(S("s3w"), S("ahi", 0, 144), col(5), None, A.is_equal)
    ts(S("bd"), S("xg"), col(2), None, A.is_equal)
    ts(col(3), col(1), -2048.0, None, A.add)
    ts(S("l1"), S("ahi", 0, 16), 0.0, col(1), A.mult, A.add)
    ts(S("c16", 1024), S("ahi"), 16.0, col(3), A.mult, A.add)
    ts(S("l1"), S("l1"), 17.0, 17.0, A.mult, A.add)
    keep(S("tri"), S("bd"), [[1, 128]], A.is_ge, -1)
    fold(0, 0, 0)
    keep(S("kp"), S("one"), [[0, 16], [1, 16]], A.not_equal, 0)
    ac(S("alo"), S("ahi"), AF.Identity, 0.0, col(1))

    def scaled(lst):
        for out, src, sc in lst:
            ac(out, src, AF.Identity if isinstance(sc, tuple) else AF.Copy, sc)
    scaled(((S("en1", 0, 128), S("e1"), -1.0), (S("gn"), S("bd", s=16), -8192.0), (S("gp"), S("bd", s=16), 8192.0),
            (S("e16"), S("e1"), 16.0), (S("ef"), S("e1"), 1.0), (S("skp"), S("s3w"), 8192.0), (S("e256"), S("e1"), 256.0),
            (S("en16", 0, 128), S("e1"), -16.0), (S("en1", 128), S("e1"), -1.0), (S("en16", 128), S("e1"), -16.0),
            (S("s1w"), S("s3w"), col(8)), (S("sxy", 0, 8), S("bd", s=16), col(8)), (S("sxy", 8), S("bd", s=16), col(11))))

    scaled(((S("nbd"), S("bd"), -1.0), (S("e17"), S("e1"), 17.0), (S("e272"), S("e1"), 272.0), (S("s4w"), S("s3w"), 16.0),
            (S("ntri"), S("tri"), -1.0)))
    ac(S("k1"), S("k1a"), AF.Identity, 1.0, col(1))

    if VO:
        tt(S("x40", 0, VO), S("z0", 0, VO), S("w", 0, VO), A.min)
    cp(S("cu"), S("ci"))
    ts(S("c16", 0, 1024), S("ci"), -2048.0, None, A.add)

    KEY = ((2048, 2176), (2560, 3072), (2688, 2816), (2048, 3200), (3712, 2432))
    KP, KF, KW, KT = 3968, 2560, 3584, 2176
    flip = [0]

    def short(src, dst, a, b):
        d = flip[0] * 1024
        flip[0] ^= 1
        for o, e in blocks(a, b, 512):
            pe([(P(d + o - a, e - o), S("e1"), S("w", o, e)), (P(d + o - a, e - o), S("en1", 0, 128), S(src, o, e))], prio=0)
        return lambda: ac(S(dst, a, b), P(d, b - a), AF.Relu)

    def sums(k, h, buf, sel):
        n = width(sel)
        return [(P(k + r, 16 * n - r, 16), S(buf, h * 2048 + r, h * 2048 + 2048, 16), sel) for r in range(16)]

    def wrap(k, src, a, b, sel):
        return [(P(k, (b - a) // 16), S(sel, 15 - r, 143 - r), S(src, a + r, b, 16)) for r in range(16)]

    def half(name, h, o=0):
        return S(name, o + h * 128, o + h * 128 + 128)

    tab = "x00"
    for t in range(2):
        z, zn = "z%d" % t, "z%d" % (t + 1)
        x = [mins(d, t) for d in range(5)]

        def turned_key(d, h, place=1, split=False):
            k = KEY[d][h]
            out = P(k, 128)
            relus = d == 2 and (2, h * 2048, h * 2048 + 1024) not in FOLDS[t]
            if relus:
                mms = [(out, S("e1"), half("whi", h)), (out, S("e1"), half("wlo", h))]
            else:
                mms = [(out, S("con", 128 - 128 * place, 256 - 128 * place, p=two), S("one", 0, 128, p=two))]
            mms.append((out, half("c16", h, d * 256), S("eh")))
            if split:
                pe(mms, last=False)
                mms = []
            pe(mms + sums(k, h, x[d], S("gp" if relus else "gn")), first=not split)

        def vmin(d, a, b):
            tt(S(x[d], a, b), ind(z, V, "cu", d * V + a, d * V + b), S("w", a, b), A.min)

        def sgather(d, a, b):
            ac(S("zg%d" % d, a, b), ind(z, V, "cu", d * V + a, d * V + b))

        def chain(h):
            def merge(dst, src, d):
                return lambda: tt(half(dst, h), half(src, h), P(KEY[d][h], 128), A.min)

            def clear():
                ts(half("bj", h), half("bi", h), -4097, None, A.bitwise_and)

            def own():
                merge("pf", "bj", 4)()
                pe([(P(KP, 128), half("pf", h), S("ef"))])

            def turn():
                cp(S("ht"), S("hti"))
                for i in range(2):
                    pe([(P(KT + i * 128, 128), half("ht", i), S("e1"))])
                for i in range(2):
                    ac(half("hl", 0, i * 256), P(KT + i * 128, 128))
            out = ("hti", "hli")[h]
            parts = [merge("bi", "bj", 3), lambda: ts(half(out, h), half("bi", h), 4, 255, A.arith_shift_right, A.bitwise_and),
                     lambda: ts(half(out, 1, 256 * h), half("bi", h), 15, None, A.bitwise_and)]
            if h == 0:
                return [merge("bi", "b0", 4), clear, merge("bi", "bj", 1), clear, merge("bi", "bj", 2), clear] + parts + [turn]
            return ([merge("bi", "b0", 1), clear, merge("bi", "bj", 2), clear, own,
                     lambda: ts(half("bi", h), P(KP, 128), 4096.0, None, A.add), clear] + parts
                    + [lambda i=i: cp(half("hl", h, i), half("hli", h, i)) for i in (0, 256)])

        relu = [None]

        def scalar_block(d=None, a=0, b=0):
            last = relu[0]
            relu[0] = None
            if d:
                sgather(d, a, b)
                if (d, a, b) not in FOLDS[t]:
                    relu[0] = short("zg%d" % d, x[d], a, b)
            if last:
                last()

        def key3():
            out = P(KEY[3][1], 128)
            pe([(out, S("eh"), half("c16", 1, 768))] + [(out, half(y, 1), S("e1")) for y in ("whi", "wlo")], last=False)

        def sum3(a, b, last=False):
            pe(wrap(KEY[3][1] - 128 + a // 16, x[3], a, b, "skp"), first=False, last=last)
        A0, B0 = chain(0), chain(1)
        for q in range(1 - t, len(FOLDS[t])):
            fold(t, q, 0)
        for a, b in blocks(0, 2048):
            scalar_block(2, a, b)
        for a, b in ((0, 768), (768, 2048)) if t == 0 else ((0, 2048),):
            vmin(0, a, b)
            vmin(1, a, b)
        if t == 0:
            pe([(P(KW, 256), S("con", 0, 128, p=two), S("one", p=two))] + sums(KW, 0, "w", S("gn")), last=False)
        turned_key(0, 0)
        if t == 0:
            pe(sums(KW + 128, 1, "w", S("gn")), first=False)
        scalar_block(2, 2048, 3072)
        turned_key(1, 0)
        if t == 0:
            vmin(0, 2048, 3072)
            ac(S("whi"), P(KW, 256))
            tt(S("wlo"), P(KW, 256), S("whi"), A.subtract)
        turned_key(2, 0)
        scalar_block(2, 3072, V)
        vmin(0, 3072 - 1024 * t, V)
        turned_key(0, 1, 0)
        if t == 0:
            move("sp", "da", S(tab, p=(2, 128, 16)), S("ahi"))
            move("sp", "db", S(tab, p=(3, 128, 16)), S("alo"))
        turned_key(4, 0, 0)
        scalar_block(3, 2048, 3072)
        vmin(1, 2048, V)
        turned_key(1, 1)
        turned_key(2, 1)
        last, relu[0] = relu[0], None
        scalar_block(3, 3072, V)
        ac(S("b0"), P(KEY[0][0], 256))
        last()
        scalar_block()
        turned_key(4, 1, -1)
        vmin(3, 0, 2048)
        turned_key(3, 0)
        A0[0]()
        B0[0]()
        key3()
        sum3(2048, 3072)
        for step in [s for pair in zip(A0[1:5], B0[1:5]) for s in pair]:
            step()
        sum3(3072, V, True)
        for step in [A0[5], A0[6], B0[5], A0[7], B0[6], A0[8], A0[9]] + B0[7:]:
            step()
        move("sp", "dh%d" % t, S(tab, p=(0, 128, 16)), S("hl", 0, 256))
        move("act", "dl%d" % t, S(tab, p=(1, 128, 16)), S("hl", 256, 512))
        pe([(P(KF, 256), S("e1"), S("hl", 0, 256)), (P(KF, 256), S("e256"), S("hl", 256, 512))])
        cp(S("lf"), P(KF, 256))
        pe([(P(0, 512, 2), S("e16"), S("ahi")), (P(0, 512, 2), S("e1"), S("alo")),
            (P(0, 512, 2), S("en16", 0, 128), S("hl", 0, 256)), (P(0, 512, 2), S("en1", 0, 128), S("hl", 256, 512))])
        pe([(P(513, 511, 2), S("e16"), S("hl", 0, 256)), (P(513, 511, 2), S("e1"), S("hl", 256, 512))])
        ac(S("di", 0, 512, 2), P(0, 512, 2))
        ac(S("di", 1, 512, 2), P(513, 511, 2))

        XY, KG, KU = (1024, 1536), (2048, 2560), (3072, 3584)
        for h in range(2):
            pe([(P(XY[h], 256), half("ahi", h), S("en16")), (P(XY[h], 256), half("alo", h), S("en1"))], last=False, prio=2)

        def both(win, lst, dst, a, n, b):
            cp(S(dst, a, a + n), ind(win, V, lst, a, a + n))
            ac(S(dst, a + n, b), ind(win, V, lst, a + n, b))
        for q, (a, b) in enumerate(blocks(0, V)):
            if q == 3:
                cp(S("lg", 0, 128), P(KG[0], 128))
            both(tab, "lf", "t2", a, G1[q], b)
            pe(wrap(KG[q // 2] + q % 2 * 64, "t2", a, b, "s1w"))
        both("t2", "lg", "t3", 0, G2[0], 2048)
        cp(S("lg", 128, 256), P(KG[1], 128))

        def differs(h):
            ts(S("nn", h * 256, h * 256 + 256), P(XY[h], 256), 0.0, None, A.not_equal)
            pe([(P(KU[h], 128), half("nn", 2 * h + i), S("e1")) for i in range(2)])

        def unmet(h):
            ts(S("fi", h * 256 + 1, h * 256 + 256, 2), P(KU[h], 128), 1.5, None, A.is_ge)

        def trades(h):
            scan(S("pp", h * 256, h * 256 + 256), S("fi", h * 256, h * 256 + 256), S("di", h * 256, h * 256 + 256), A.mult, A.add)

        def trade_list(h):
            cp(half("lp", h), S("pp", h * 256 + 1, h * 256 + 256, 2))
        pe(sums(XY[0], 0, "t3", S("sxy")), first=False)
        m = 2048 + G2[1] + G2[2]
        ac(S("t3", m, V), ind("t2", V, "lg", m, V))
        cp(S("t3", 2048, 2048 + G2[1]), ind("t2", V, "lg", 2048, 2048 + G2[1]))
        differs(0)
        cp(S("t3", 2048 + G2[1], m), ind("t2", V, "lg", 2048 + G2[1], m))
        pe(sums(XY[1], 1, "t3", S("sxy")), first=False)
        unmet(0)
        trades(0)
        KN = (0, 512)
        pe([(P(KN[0], 128), S("bd"), S("fi", 1, 256, 2))])
        pe([(P(KN[1] + 128, 16), S("bd"), S("one", 0, 16)), (P(KN[1] + 128, 16), S("nbd"), S("fi", 1, 32, 2))])
        differs(1)
        trade_list(0)
        ac(S(zn, 0, 2048), ind(z, V, "lp", 0, 2048))
        scan(S("eb", 1, 129), P(KN[0], 128), S("c256", 0, 128), A.add, A.min)
        unmet(1)
        pe([(P(KN[1], 128), S("bd"), S("fi", 257, 512, 2))])
        pe([(P(XY[0], 256), S("tri"), S("fi", 1, 512, 2))])
        pe([(P(XY[0] + 256, 16), S("tri"), S("one", 0, 16)), (P(XY[0] + 256, 16), S("ntri"), S("fi", 1, 32, 2))])
        scan(S("eb", 129, 273), P(KN[1], 144), S("c256", 0, 144), A.add, A.min, S("eb", 128, 129))
        pe([(P(KG[0], 16), S("s3w", 15 - r, 143 - r), S("eb", 1 + r, 1 + r + 256, 17)) for r in range(16)])
        tt(S("m1"), ind("eb", 273, "l1", 0, 256), S("k1"), A.is_le)
        ts(S("tb"), P(KG[0], 16), 0.0625, None, A.mult)
        scan(S("s1"), S("kp"), S("m1"), A.mult, A.add)
        cp(S("l2"), S("s1", 15, 256, 16))
        tt(S("m2"), ind("tb", 16, "l2", 0, 256), S("ahi"), A.is_le)
        KC, KV = KG[1], KU[0]
        pe([(P(KC, 16), S("e17"), S("s1", 15, 256, 16))], last=False)
        pe([(P(KV, 16), S("e272"), S("s1", 15, 256, 16))], last=False)
        pe(wrap(KC, "m2", 0, 256, "s3w"), first=False, prio=0)
        pe(wrap(KV, "m2", 0, 256, "s4w"), first=False, last=False)
        trades(1)
        tt(S("pin"), S("eb", 0, 272), P(XY[0], 272), A.add)
        cp(S("l3"), P(KC, 16))
        tt(S("m3"), ind("pin", 272, "l3", 0, 256), S("ahi"), A.is_le)
        pe(wrap(KV, "m3", 0, 256, "s3w"), first=False)
        trade_list(1)
        ac(S(zn, 2048, ZS), ind(z, V, "lp", 2048, ZS))
        cp(S(z, V, V + 256), ind(z, V, "lp", 0, 256))
        cp(S("lv"), P(KV, 16))
        away, land = S("away%d" % t), S("land%d" % t)
        cp(away, ind(z, V + 256, "lv", 0, 256))
        dst = T.cores[(rank + 1 + t) % n_ranks]
        eng = topo.engines(core, dst)
        got = len(topo.engines(T.cores[(rank - 1 - t) % n_ranks], core))
        net = ("net%d" % t, 0, 1, 1, 0, 1, 1)

        def send(g, t=t, dst=dst, eng=eng, away=away, land=land):
            rid, pid, _ = topo.addr(dst)
            g.remote_dma(ap(land), ap(away), T.sem["arr%d" % t], T.sem["sent"], pid, rid, sum(1 << e for e in eng))
            return None
        add("pool", send, [away], [net], 0.1, sem="sent", lat=ROWS + 65536 / DRATE, inc=len(eng))
        add("net", None, [net], [land], 0.0, sem="arr%d" % t, inc=got)
        cp(S("oi"), P(KV, 16))
        cp(S(zn, ZS, V), ind(z, V, "lp", ZS, V))
        ts(S("oj"), S("oi"), 4095, None, A.bitwise_and)
        cp(S("lo"), S("oj"))
        cp(ind(zn, V, "lo", 0, 256), land)
    dma("sp", "dy0", T.y[:], T.z2[:], [S("z2")], [("y", 0, 1, 1, 0, 1, 1)], 1024e3)
    return ops


def _meet(x, y):
    if x[0] != y[0] or x[1] >= y[2] or y[1] >= x[2] or (x[3] == y[3] and (x[1] - y[1]) % x[3]):
        return False
    return not (x[6] == y[6] and (x[4] - y[4]) % x[6])


def _banks(o):
    s = set()
    for r in o["rd"] + o["wr"]:
        if r[0] == "ps":
            s.update(range(r[1] // 512, (r[2] - 1) // 512 + 1))
    return s


def order(ops):
    n = len(ops)
    banks = [_banks(o) for o in ops]
    names = [(set(x[0] for x in o["wr"]), set(x[0] for x in o["rd"] + o["wr"])) for o in ops]
    deps = [[] for _ in ops]
    prev = [None] * n
    last = {}
    for j in range(n):
        b = ops[j]
        if b["q"] not in LOOSE:
            prev[j] = last.get(b["q"])
            last[b["q"]] = j
        for i in range(j):
            a = ops[i]
            if banks[i] & banks[j] and a["q"] == b["q"] == "pe" and (a["part"] or b["part"]):
                deps[j].append(i)
            elif (names[i][0] & names[j][1] or names[i][1] & names[j][0]) and (
                    any(_meet(x, y) for x in a["wr"] for y in b["rd"] + b["wr"]) or any(_meet(x, y) for x in a["rd"] for y in b["wr"])):
                deps[j].append(i)
    seq, best = list(range(n)), None
    if not PASSES:
        return seq, [deps[j] + [i for i in range(j) if banks[i] & banks[j] and ops[i]["q"] != ops[j]["q"]] for j in seq]
    for again in range(PASSES):
        rest = [0.0] * n
        behind = {}
        for j in reversed(seq):
            q = ops[j]["q"]
            if q != "net" and (again or q != "pe"):
                rest[j] = max(rest[j], behind.get(q, 0.0))
            rest[j] += ops[j]["cost"]
            behind[q] = rest[j]
            rest[j] += DLAT + ops[j]["lat"] if ops[j]["sem"] and q != "net" else 0.0
            for i in deps[j]:
                rest[i] = max(rest[i], rest[j] + WAKE)
        user = {}

        def others(j):
            return [i for (b, q), i in user.items() if b in banks[j] and q != ops[j]["q"]]
        done = [None] * n
        free = {}
        ring = 0.0
        seq, full = [], [None] * n
        left = list(range(n))
        while left:
            ready = []
            for j in left:
                if (prev[j] is not None and done[prev[j]] is None) or any(done[i] is None for i in deps[j]):
                    continue
                st = max([free.get(ops[j]["q"], 0.0)]
                         + [done[i] + (0 if ops[i]["q"] == ops[j]["q"] == "pe" else WAKE) for i in deps[j] + others(j)])
                ready.append((st, j))
            st, j = min(ready)
            q = ops[j]["q"]
            st, j = max([x for x in ready if x[0] <= st + AHEAD and ops[x[1]]["q"] == q], key=lambda x: rest[x[1]] - x[0])
            o = ops[j]
            full[j] = deps[j] + others(j)
            for b in banks[j]:
                user[b, q] = j
            if q != "net":
                free[q] = st + o["cost"]
            if o["sem"] and q != "net":
                ring = max(ring, st + (RLAT if q == "pool" else DLAT)) + o["lat"]
                done[j] = ring
            else:
                done[j] = st + o["cost"]
            left.remove(j)
            seq.append(j)
        if best is None or max(done) < best[0]:
            best = (max(done), seq, full)
    return best[1:]


def hand_back(g, core, home, T, topo):
    rid, pid, _ = topo.addr(home)
    eng = topo.engines(core, home)
    for t in range(2):
        for q, (d, a, b) in enumerate(FOLDS[t]):
            x = T[mins(d, t)][:, a:b]
            g.wait_ge(T.sem["out%d%d" % (t, q)], len(topo.engines(home, core)))
            g.remote_dma(x, x, T.sem["back%d%d" % (t, q)], T.sem["sent"], pid, rid, sum(1 << e for e in eng))
    g.wait_ge(T.sem["sent"], sum(len(x) for x in FOLDS) * len(eng))


def rank_program(g, core, T, topo):
    if T.rank_of(core) is None:
        for home, h in helpers(T, topo).items():
            if h == core:
                hand_back(g, core, home, T, topo)
        return
    ops = plan(T, topo, core)
    seq, deps = order(ops)
    queue = {"pe": g.tensor, "dve": g.vector, "act": g.scalar, "pool": g, "sp": g.sync}
    place = {j: k for k, j in enumerate(seq)}
    seen = {q: {} for q in list(queue) + ["net"]}
    after = {}
    waits = {}
    for j in seq:
        o = ops[j]
        know = seen[o["q"]]
        need = []
        for i in sorted(deps[j], key=lambda i: -place[i]):
            a = ops[i]
            if o["q"] == "net" or (a["q"] == "pe" and o["q"] == "pe"):
                continue
            if know.get(a["sem"] or a["q"], -1) >= place[i]:
                continue
            need.append(i)
            for k, v in after[i].items():
                know[k] = max(know.get(k, -1), v)
        waits[j] = need
        after[j] = {} if o["q"] == "net" else dict(know)
        after[j][o["sem"] or o["q"]] = place[j]
    marked = set(i for j in seq for i in waits[j])
    count = {}
    value = {}
    for j in seq:
        o = ops[j]
        if o["sem"] or j in marked:
            s = o["sem"] or o["q"]
            count[s] = count.get(s, 0) + (o["inc"] if o["sem"] else 1)
            value[j] = (s, count[s])
    for j in seq:
        o = ops[j]
        if o["q"] == "net":
            continue
        for i in waits[j]:
            queue[o["q"]].wait_ge(T.sem[value[i][0]], value[i][1])
        ins = o["fn"](g)
        if j in value and ins is not None:
            ins.then_inc(T.sem[value[j][0]], 16 if o["sem"] else 1)
    for s in sorted(count, key=lambda s: s.startswith("dy")):
        g.wait_ge(T.sem[s], count[s])
